import numpy as np
import ml_dtypes


def mxq(x, axis, fmt="e4m3"):
    dtype, down = {"e4m3": (ml_dtypes.float8_e4m3fn, 7), "e5m2": (ml_dtypes.float8_e5m2, 14)}[fmt]
    v = np.moveaxis(np.asarray(x, np.float32).astype(ml_dtypes.bfloat16).astype(np.float64), axis, -1)
    blocks = v.reshape(v.shape[:-1] + (-1, 32))
    amax = np.abs(blocks).max(-1, keepdims=True)
    byte = np.maximum(np.where(amax > 0, np.frexp(amax)[1] - 1 + 127, 0) - down, 1)
    scale = np.exp2(byte - 127.0)
    codes = (blocks / scale).astype(np.float32).astype(dtype).astype(np.float64)
    return np.moveaxis((codes * scale).reshape(v.shape), -1, axis)


WIDE = False


def mx_kscale(k):
    if not WIDE:
        return np.ones(k)
    levels = np.array([10, -10, 5, -5, 0])
    if k % 512:
        return np.exp2(np.random.permutation(np.resize(levels, k // 32))).repeat(32)
    a = np.empty((k // 512, 16))
    for p in range(k // 512):
        a[p, :8] = np.random.permutation(np.resize(levels, 8))
        for g in range(8):
            far = levels[np.abs(levels - a[p, g]) >= 10]
            a[p, g + 8] = far[np.random.randint(len(far))]
    return np.exp2(a.ravel()).repeat(32)


def f64(x):
    return np.asarray(x).astype(np.float64)


def striped(idx):
    return np.tile(np.asarray(idx).reshape(-1, 16).T, (8, 1)).astype(np.uint16)


def unstriped(offs):
    return offs[:16].T.reshape(-1).astype(np.int64)


E2M1 = np.array([0.0, 0.5, 1.0, 1.5, 2.0, 3.0, 4.0, 6.0, -0.0, -0.5, -1.0, -1.5, -2.0, -3.0, -4.0, -6.0])


def pack_weight(w, fmt):
    k, n = w.shape
    w = f64(np.asarray(w, np.float32).astype(ml_dtypes.bfloat16)).reshape(k // 32, 32, n)
    amax = np.abs(w).max(1)
    if fmt == "e4m3":
        byte = np.frexp(amax)[1] - 1 + 127 - 7
    else:
        mant, ex = np.frexp(amax / 6.0)
        byte = np.where(mant > 0.5, ex, ex - 1) + 127
    byte = np.clip(np.where(amax > 0, byte, 1), 1, 254)
    scaled = (w * np.exp2(127.0 - byte)[:, None, :]).reshape(k, n).astype(np.float32)
    by_word = np.ascontiguousarray(scaled.reshape(k // 512, 128, 4, n).transpose(0, 1, 3, 2))
    if fmt == "e4m3":
        words = by_word.astype(ml_dtypes.float8_e4m3fn).view(np.uint8)
    else:
        c = by_word.astype(ml_dtypes.float4_e2m1fn).view(np.uint8) & 0xF
        words = (c[..., 0::2] | (c[..., 1::2] << 4)).reshape(k // 512, 128, 2 * n)
    return np.ascontiguousarray(words), np.ascontiguousarray(byte.astype(np.uint8).reshape(k // 512, 16, n))


def unpack_weight(words, scales, fmt):
    g, _, n = scales.shape
    words = np.ascontiguousarray(words).reshape(g, 128, n, -1)
    if fmt == "e4m3":
        vals = words.view(ml_dtypes.float8_e4m3fn).astype(np.float64)
    else:
        nib = np.empty((g, 128, n, 4), np.uint8)
        nib[..., 0::2] = words & 0xF
        nib[..., 1::2] = words >> 4
        vals = E2M1[nib]
    vals = vals * np.repeat(np.exp2(scales.astype(np.float64) - 127.0), 8, axis=1)[..., None]
    return vals.transpose(0, 1, 3, 2).reshape(g * 512, n)


B, N, T, D, DV, NQ = 1, 1024, 2048, 1024, 128, 256


def setup_inputs():
    n = np.random.standard_normal
    idx = np.sort(np.random.permutation(T)[:B * N].reshape(B, N), axis=1).reshape(-1)
    s = mx_kscale(D)[:, None]
    u = np.ones(T)
    u[idx] = mx_kscale(B * N)
    r = np.random.uniform(0.5, 2.0, T)
    qp = [pack_weight(x, "e4m3") for x in n((B, D, NQ)) * s * (0.80 / np.sqrt(D))]
    k = n((D, T)) / s
    v = n((DV, T)) / (u * r)
    kp = pack_weight(k, "e2m1")
    return {
        "q_words": np.stack([x[0] for x in qp]),
        "q_scales": np.stack([x[1] for x in qp]),
        "k_words": np.ascontiguousarray(kp[0].reshape(D // 1024, 2, 128, T, 2).transpose(0, 2, 3, 1, 4)).reshape(D // 1024, 128, T, 4),
        "k_scales": kp[1],
        "vT": v.astype(np.float32),
        "vs": np.tile(u * r, (128, 1)).astype(np.float32),
        "kb": np.tile(n(T), (128, 1)).astype(np.float32),
        "og": n((B, NQ, DV)).astype(np.float32),
        "offs": striped(idx),
    }


def reference(q_words, q_scales, k_words, k_scales, vT, vs, kb, og, offs):
    idx = unstriped(offs)
    k = unpack_weight(k_words.reshape(D // 1024, 128, T, 2, 2).transpose(0, 3, 1, 2, 4).reshape(D // 512, 128, 2 * T), k_scales, "e2m1")
    v = f64(vT)
    pick = lambda x: x[:, idx].reshape(x.shape[0], B, N).transpose(1, 0, 2)
    q = np.stack([unpack_weight(q_words[b], q_scales[b], "e4m3") for b in range(B)])
    score = q.transpose(0, 2, 1) @ pick(k)
    score = score + pick(f64(kb))[:, :1, :]
    p = 1.0 / (1.0 + np.exp(-score))
    w = p * pick(f64(vs))[:, :1, :]
    y = mxq(w, 2, "e4m3") @ mxq(pick(v).transpose(0, 2, 1), 1, "e4m3")
    y = y / 16.0
    y = y / (1.0 + np.exp(-f64(og)))
    return y

@@ -1,0 +1,199 @@
+from contextlib import ExitStack
+
+import concourse.mybir as mybir
+from concourse.masks import make_identity
+
+N, T, D, DV, NQ = 1024, 2048, 1024, 128, 256
+FLOPS = 2 * NQ * N * (D + DV)
+
+F32 = mybir.dt.float32
+BF16 = mybir.dt.bfloat16
+I32 = mybir.dt.int32
+U32 = mybir.dt.uint32
+U16 = mybir.dt.uint16
+U8 = mybir.dt.uint8
+FP8X4 = mybir.dt.float8_e4m3fn_x4
+FP4X4 = mybir.dt.float4_e2m1fn_x4
+MULT = mybir.AluOpType.mult
+SIGMOID = mybir.ActivationFunctionType.Sigmoid
+COPY = mybir.ActivationFunctionType.Copy
+
+P = 128
+PACK = 4
+PASS = P * PACK
+DP = D // PASS
+SP = N // PASS
+QH = NQ // P
+COLS = PASS // 16
+
+
+def tile_attend_sigm_kb_gate_srtq256n1024t2048_kernel(
+    tc, q_words, q_scales, k_words, k_scales, vT, vs, kb, og, offs, out
+):
+    nc = tc.nc
+    with ExitStack() as ctx:
+        keep = ctx.enter_context(tc.tile_pool(name="keep", bufs=1))
+        score_ps = ctx.enter_context(tc.psum_pool(name="score_ps", bufs=4))
+        turn_ps = ctx.enter_context(tc.psum_pool(name="turn_ps", bufs=4))
+
+        offsets = keep.tile([P, N // 16], U16, name="offsets")
+        kw_win = keep.tile([P, T], U32, name="kw_win")
+        ks_win = keep.tile([P, DP, T], U8, name="ks_win")
+        kb_win = keep.tile([P, T], F32, name="kb_win")
+        vs_win = keep.tile([P, T], F32, name="vs_win")
+        v_raw = keep.tile([P, T], F32, name="v_raw")
+        v_win = keep.tile([P, T], BF16, name="v_win")
+        q_codes = keep.tile([P, DP, NQ], U32, name="q_codes", align_bytes=64)
+        q_plane = keep.tile([P, DP, NQ], U8, name="q_plane", align_bytes=64)
+        og_raw = keep.tile([P, QH, DV], F32, name="og_raw")
+        gate = keep.tile([P, QH, DV], F32, name="gate")
+        ident = keep.tile([P, P], F32, name="ident")
+
+        nc.sync.dma_start(offsets[:], offs)
+        nc.sync.dma_start(kw_win[:].bitcast(I32), k_words[0].rearrange("p t b -> p (t b)").bitcast(I32))
+        nc.vector.memset(ks_win[:].bitcast(I32), 0)
+        for quad in range(4):
+            nc.scalar.dma_start(
+                ks_win[32 * quad : 32 * quad + 4, :, :].bitcast(I32),
+                k_scales[:, 4 * quad : 4 * quad + 4, :].rearrange("o f t -> f o t").bitcast(I32),
+            )
+        nc.vector.memset(kb_win[:], 0.0)
+        nc.scalar.dma_start(kb_win[0:1, :], kb[0:1, :])
+        nc.sync.dma_start(q_codes[:].bitcast(I32), q_words[0].rearrange("o p q r -> p o (q r)").bitcast(I32))
+        nc.sync.dma_start(v_raw[:], vT)
+        nc.vector.memset(vs_win[:], 0.0)
+        nc.sync.dma_start(vs_win[0:1, :], vs[0:1, :])
+
+        nc.gpsimd.dma_start(og_raw[:], og[0].rearrange("(h p) e -> p h e", p=P))
+        nc.gpsimd.memset(q_plane[:].bitcast(I32), 0)
+        for quad in range(4):
+            nc.gpsimd.dma_start(
+                q_plane[32 * quad : 32 * quad + 4, :, :].bitcast(I32),
+                q_scales[0][:, 4 * quad : 4 * quad + 4, :].rearrange("o f q -> f o q").bitcast(I32),
+            )
+        make_identity(nc, ident[:])
+
+        nc.scalar.activation(gate[:], og_raw[:], SIGMOID)
+        nc.scalar.copy(v_win[:], v_raw[:])
+
+        def lists(u):
+            return offsets[:, u * COLS : (u + 1) * COLS]
+
+        kw_got = [keep.tile([P, PACK, P], U32, name="kw_got%d" % u) for u in range(SP)]
+        ks_got = [keep.tile([P, DP, PASS], U8, name="ks_got%d" % u) for u in range(SP)]
+        kb_got = [keep.tile([P, PASS], F32, name="kb_got%d" % u) for u in range(SP)]
+        vs_got = [keep.tile([P, PASS], F32, name="vs_got%d" % u) for u in range(SP)]
+        k_codes = [keep.tile([P, DP, 2 * PASS], U8, name="k_codes%d" % u, align_bytes=64) for u in range(SP)]
+        k_plane = [keep.tile([P, DP, PASS], U8, name="k_plane%d" % u, align_bytes=64) for u in range(SP)]
+        kb_col = [keep.tile([P, PACK], F32, name="kb_col%d" % u) for u in range(SP)]
+        vs_col = [keep.tile([P, PACK], F32, name="vs_col%d" % u) for u in range(SP)]
+        prob = [keep.tile([P, PACK, NQ], F32, name="prob%d" % u) for u in range(SP)]
+        w_bf = [keep.tile([P, NQ, PACK], BF16, name="w_bf%d" % u, align_bytes=64) for u in range(SP)]
+        w_codes = [keep.tile([P, NQ], U32, name="w_codes%d" % u, align_bytes=64) for u in range(SP)]
+        w_plane = [keep.tile([P, NQ], U8, name="w_plane%d" % u, align_bytes=64) for u in range(SP)]
+        v_got = keep.tile([P, SP, 2, P, 2], BF16, name="v_got")
+        v_bf = keep.tile([P, SP, DV, PACK], BF16, name="v_bf", align_bytes=64)
+        v_codes = keep.tile([P, SP, DV], U32, name="v_codes", align_bytes=64)
+        v_plane = keep.tile([P, SP, DV], U8, name="v_plane", align_bytes=64)
+
+        def to_columns(got, col):
+            turned = turn_ps.tile([P, PACK, P], F32, name="turned", tag="turn")
+            for t in range(PACK):
+                nc.tensor.transpose(turned[:, t, :], got[:, t::PACK], ident[:])
+            nc.scalar.copy(col[:], turned[:, :, 0])
+
+        def keys(u):
+            nc.vector.tensor_copy(kw_got[u][:].rearrange("g t p -> g p t"), kw_win[:].indirect(lists(u)))
+            nc.vector.tensor_copy(ks_got[u][:, 0, :], ks_win[:, 0, :].indirect(lists(u)))
+            nc.vector.tensor_copy(
+                k_codes[u][:].bitcast(U16),
+                kw_got[u][:].rearrange("g t p -> g (t p)").bitcast(U16).rearrange("g (s o) -> g o s", o=DP),
+            )
+            nc.vector.tensor_copy(ks_got[u][:, 1, :], ks_win[:, 1, :].indirect(lists(u)))
+            nc.vector.tensor_copy(kb_got[u][:], kb_win[:].indirect(lists(u)))
+            nc.vector.tensor_copy(
+                k_plane[u][:].rearrange("g o (t p) -> g o t p", t=PACK),
+                ks_got[u][:].rearrange("g o (p t) -> g o t p", t=PACK),
+            )
+            to_columns(kb_got[u], kb_col[u])
+
+        def scores(u):
+            for pair in range(PACK // 2):
+                bank = score_ps.tile([P, 2, NQ], F32, name="bank", tag="score")
+                for e in range(2):
+                    t = 2 * pair + e
+                    for h in range(QH):
+                        for o in range(DP):
+                            nc.tensor.matmul_mx(
+                                out=bank[:, e, h * P : (h + 1) * P],
+                                lhsT=k_codes[u][:, o, 2 * P * t : 2 * P * (t + 1)].bitcast(FP4X4),
+                                lhsT_scale=k_plane[u][:, o, P * t : P * (t + 1)],
+                                rhs=q_codes[:, o, h * P : (h + 1) * P].bitcast(FP8X4),
+                                rhs_scale=q_plane[:, o, h * P : (h + 1) * P],
+                                start=(o == 0),
+                                stop=(o == DP - 1),
+                            )
+                for e in range(2):
+                    t = 2 * pair + e
+                    nc.scalar.activation(prob[u][:, t, :], bank[:, e, :], SIGMOID, bias=kb_col[u][:, t : t + 1])
+
+        def values():
+            for u in range(SP):
+                nc.scalar.activation(v_got[:, u].rearrange("e h p r -> e p h r"), v_win[:].indirect(lists(u)), COPY)
+            turned = turn_ps.tile([P, SP, 2, DV], F32, name="turned_v", tag="turn")
+            for u in range(SP):
+                for h in range(2):
+                    nc.tensor.transpose(
+                        turned[:, u, h, :], v_got[:, u, h].rearrange("e p r -> e (p r)").bitcast(F32), ident[:]
+                    )
+            nc.scalar.copy(v_bf[:].bitcast(F32), turned[:].rearrange("p u h e -> p u e h"))
+
+        def weights(u, h):
+            cols = slice(h * P, (h + 1) * P)
+            nc.vector.tensor_tensor(
+                w_bf[u][:, cols, :].rearrange("p (c i) t -> p c t i", i=4),
+                prob[u][:, :, cols].rearrange("p t (c i) -> p c t i", i=4),
+                vs_col[u][:].unsqueeze(1).unsqueeze(3).to_broadcast([P, P // 4, PACK, 4]),
+                MULT,
+            )
+
+        def quantise_w(u, h):
+            cols = slice(h * P, (h + 1) * P)
+            nc.vector.quantize_mx(
+                out=w_codes[u][:, cols].bitcast(FP8X4),
+                scales=w_plane[u][:, cols],
+                in_=w_bf[u][:, cols, :].rearrange("p q t -> p (q t)"),
+            )
+
+        keys(0)
+        scores(0)
+        values()
+        keys(1)
+        for u in range(SP):
+            nc.vector.tensor_copy(vs_got[u][:], vs_win[:].indirect(lists(u)))
+            to_columns(vs_got[u], vs_col[u])
+        scores(1)
+        nc.vector.quantize_mx(
+            out=v_codes[:].rearrange("p u e -> p (u e)").bitcast(FP8X4),
+            scales=v_plane[:].rearrange("p u e -> p (u e)"),
+            in_=v_bf[:].rearrange("p u e t -> p (u e t)"),
+        )
+        acc = [turn_ps.tile([P, DV], F32, name="acc%d" % h, tag="turn") for h in range(QH)]
+        result = [keep.tile([P, DV], F32, name="result%d" % h) for h in range(QH)]
+        for u in range(SP):
+            for h in range(QH):
+                weights(u, h)
+            for h in range(QH):
+                quantise_w(u, h)
+                nc.tensor.matmul_mx(
+                    out=acc[h][:],
+                    lhsT=w_codes[u][:, h * P : (h + 1) * P].bitcast(FP8X4),
+                    lhsT_scale=w_plane[u][:, h * P : (h + 1) * P],
+                    rhs=v_codes[:, u, :].bitcast(FP8X4),
+                    rhs_scale=v_plane[:, u, :],
+                    start=(u == 0),
+                    stop=(u == SP - 1),
+                )
+        for h in range(QH):
+            nc.vector.scalar_tensor_tensor(result[h][:], acc[h][:], 1.0 / 16.0, gate[:, h, :], MULT, MULT)
+            nc.sync.dma_start(out[0, h * P : (h + 1) * P, :], result[h][:])

@@ -25,6 +25,7 @@ DP = D // PASS
 SP = N // PASS
 QH = NQ // P
 COLS = PASS // 16
+REACH = T - N + PASS
 
 
 def tile_attend_sigm_kb_gate_srtq256n1024t2048_kernel(
@@ -33,12 +34,12 @@ def tile_attend_sigm_kb_gate_srtq256n1024t2048_kernel(
     nc = tc.nc
     with ExitStack() as ctx:
         keep = ctx.enter_context(tc.tile_pool(name="keep", bufs=1))
-        score_ps = ctx.enter_context(tc.psum_pool(name="score_ps", bufs=4))
-        turn_ps = ctx.enter_context(tc.psum_pool(name="turn_ps", bufs=4))
+        score_ps = ctx.enter_context(tc.psum_pool(name="score_ps", bufs=2))
+        turn_ps = ctx.enter_context(tc.psum_pool(name="turn_ps", bufs=3))
 
         offsets = keep.tile([P, N // 16], U16, name="offsets")
         kw_win = keep.tile([P, T], U32, name="kw_win")
-        ks_win = keep.tile([P, DP, T], U8, name="ks_win")
+        ks_win = keep.tile([P, T], U8, name="ks_win")
         kb_win = keep.tile([P, T], F32, name="kb_win")
         vs_win = keep.tile([P, T], F32, name="vs_win")
         v_raw = keep.tile([P, T], F32, name="v_raw")
@@ -49,42 +50,43 @@ def tile_attend_sigm_kb_gate_srtq256n1024t2048_kernel(
         gate = keep.tile([P, QH, DV], F32, name="gate")
         ident = keep.tile([P, P], F32, name="ident")
 
-        nc.sync.dma_start(offsets[:], offs)
-        nc.sync.dma_start(kw_win[:].bitcast(I32), k_words[0].rearrange("p t b -> p (t b)").bitcast(I32))
-        nc.vector.memset(ks_win[:].bitcast(I32), 0)
-        for quad in range(4):
-            nc.scalar.dma_start(
-                ks_win[32 * quad : 32 * quad + 4, :, :].bitcast(I32),
-                k_scales[:, 4 * quad : 4 * quad + 4, :].rearrange("o f t -> f o t").bitcast(I32),
-            )
-        nc.vector.memset(kb_win[:], 0.0)
-        nc.scalar.dma_start(kb_win[0:1, :], kb[0:1, :])
-        nc.sync.dma_start(q_codes[:].bitcast(I32), q_words[0].rearrange("o p q r -> p o (q r)").bitcast(I32))
-        nc.sync.dma_start(v_raw[:], vT)
-        nc.vector.memset(vs_win[:], 0.0)
-        nc.sync.dma_start(vs_win[0:1, :], vs[0:1, :])
+        ks_got = keep.tile([P, N], U8, name="ks_got")
+        ks_laid = keep.tile([P, N], U8, name="ks_laid")
+        k_plane = keep.tile([P, DP, N], U8, name="k_plane", align_bytes=64)
 
-        nc.gpsimd.dma_start(og_raw[:], og[0].rearrange("(h p) e -> p h e", p=P))
         nc.gpsimd.memset(q_plane[:].bitcast(I32), 0)
+        make_identity(nc, ident[:])
+        nc.sync.dma_start(offsets[:], offs)
+        nc.sync.dma_start(
+            ks_win[:].bitcast(I32),
+            k_scales.rearrange("o f t -> (o f) t").bitcast(I32).unsqueeze(1).to_broadcast([32, 4, T // 4]),
+        )
+        nc.sync.dma_start(og_raw[:], og[0].rearrange("(h p) e -> p h e", p=P))
         for quad in range(4):
-            nc.gpsimd.dma_start(
+            nc.sync.dma_start(
                 q_plane[32 * quad : 32 * quad + 4, :, :].bitcast(I32),
                 q_scales[0][:, 4 * quad : 4 * quad + 4, :].rearrange("o f q -> f o q").bitcast(I32),
             )
-        make_identity(nc, ident[:])
+        nc.sync.dma_start(v_raw[:, : T // 2], vT[:, : T // 2])
+        nc.sync.dma_start(v_raw[:, T // 2 :], vT[:, T // 2 :])
+        nc.vector.memset(kb_win[:], 0.0)
+        nc.sync.dma_start(kb_win[0:1, :], kb[0:1, :])
+        nc.vector.memset(vs_win[:], 0.0)
+        nc.sync.dma_start(vs_win[0:1, :], vs[0:1, :])
+        k_rows = k_words[0].rearrange("p t b -> p (t b)").bitcast(I32)
+        nc.sync.dma_start(kw_win[:, :REACH].bitcast(I32), k_rows[:, :REACH])
+        nc.sync.dma_start(q_codes[:].bitcast(I32), q_words[0].rearrange("o p q r -> p o (q r)").bitcast(I32))
+        nc.sync.dma_start(kw_win[:, REACH:].bitcast(I32), k_rows[:, REACH:])
 
         nc.scalar.activation(gate[:], og_raw[:], SIGMOID)
-        nc.scalar.copy(v_win[:], v_raw[:])
+        nc.scalar.copy(v_win[:, : T // 2], v_raw[:, : T // 2])
+        nc.scalar.copy(v_win[:, T // 2 :], v_raw[:, T // 2 :])
 
         def lists(u):
             return offsets[:, u * COLS : (u + 1) * COLS]
 
-        kw_got = [keep.tile([P, PACK, P], U32, name="kw_got%d" % u) for u in range(SP)]
-        ks_got = [keep.tile([P, DP, PASS], U8, name="ks_got%d" % u) for u in range(SP)]
-        kb_got = [keep.tile([P, PASS], F32, name="kb_got%d" % u) for u in range(SP)]
-        vs_got = [keep.tile([P, PASS], F32, name="vs_got%d" % u) for u in range(SP)]
+        kw_got = [keep.tile([P, PACK, P], U32, name="kw_got%d" % u, tag="got%d" % u, align_bytes=64) for u in range(SP)]
         k_codes = [keep.tile([P, DP, 2 * PASS], U8, name="k_codes%d" % u, align_bytes=64) for u in range(SP)]
-        k_plane = [keep.tile([P, DP, PASS], U8, name="k_plane%d" % u, align_bytes=64) for u in range(SP)]
         kb_col = [keep.tile([P, PACK], F32, name="kb_col%d" % u) for u in range(SP)]
         vs_col = [keep.tile([P, PACK], F32, name="vs_col%d" % u) for u in range(SP)]
         prob = [keep.tile([P, PACK, NQ], F32, name="prob%d" % u) for u in range(SP)]
@@ -93,49 +95,61 @@ def tile_attend_sigm_kb_gate_srtq256n1024t2048_kernel(
         w_plane = [keep.tile([P, NQ], U8, name="w_plane%d" % u, align_bytes=64) for u in range(SP)]
         v_got = keep.tile([P, SP, 2, P, 2], BF16, name="v_got")
         v_bf = keep.tile([P, SP, DV, PACK], BF16, name="v_bf", align_bytes=64)
-        v_codes = keep.tile([P, SP, DV], U32, name="v_codes", align_bytes=64)
         v_plane = keep.tile([P, SP, DV], U8, name="v_plane", align_bytes=64)
 
         def to_columns(got, col):
-            turned = turn_ps.tile([P, PACK, P], F32, name="turned", tag="turn")
-            for t in range(PACK):
-                nc.tensor.transpose(turned[:, t, :], got[:, t::PACK], ident[:])
-            nc.scalar.copy(col[:], turned[:, :, 0])
+            nc.sync.dma_start(col[:], got[0:1, :].rearrange("o (p t) -> o p t", t=PACK))
 
-        def keys(u):
-            nc.vector.tensor_copy(kw_got[u][:].rearrange("g t p -> g p t"), kw_win[:].indirect(lists(u)))
-            nc.vector.tensor_copy(ks_got[u][:, 0, :], ks_win[:, 0, :].indirect(lists(u)))
+        def key_scales():
+            nc.vector.tensor_copy(ks_got[:], ks_win[:].indirect(offsets[:]))
+            nc.vector.memset(k_plane[:].bitcast(I32), 0)
+            nc.vector.tensor_copy(
+                ks_laid[:].rearrange("g (u t p) -> g u t p", u=SP, t=PACK),
+                ks_got[:].rearrange("g (u p t) -> g u t p", u=SP, t=PACK),
+            )
+            for o in range(DP):
+                for quad in range(4):
+                    first = 64 * o + 16 * quad
+                    nc.sync.dma_start(
+                        k_plane[32 * quad : 32 * quad + 4, o, :].bitcast(I32),
+                        ks_laid[first : first + 16 : 4, :].bitcast(I32),
+                    )
+
+        def key_words(u):
+            nc.vector.tensor_copy(kw_got[u][:].rearrange("g t p -> g p t"), kw_win[:, : (REACH, T)[u]].indirect(lists(u)))
+
+        def part_words(u):
             nc.vector.tensor_copy(
                 k_codes[u][:].bitcast(U16),
                 kw_got[u][:].rearrange("g t p -> g (t p)").bitcast(U16).rearrange("g (s o) -> g o s", o=DP),
             )
-            nc.vector.tensor_copy(ks_got[u][:, 1, :], ks_win[:, 1, :].indirect(lists(u)))
-            nc.vector.tensor_copy(kb_got[u][:], kb_win[:].indirect(lists(u)))
-            nc.vector.tensor_copy(
-                k_plane[u][:].rearrange("g o (t p) -> g o t p", t=PACK),
-                ks_got[u][:].rearrange("g o (p t) -> g o t p", t=PACK),
-            )
-            to_columns(kb_got[u], kb_col[u])
 
-        def scores(u):
-            for pair in range(PACK // 2):
-                bank = score_ps.tile([P, 2, NQ], F32, name="bank", tag="score")
-                for e in range(2):
-                    t = 2 * pair + e
-                    for h in range(QH):
-                        for o in range(DP):
-                            nc.tensor.matmul_mx(
-                                out=bank[:, e, h * P : (h + 1) * P],
-                                lhsT=k_codes[u][:, o, 2 * P * t : 2 * P * (t + 1)].bitcast(FP4X4),
-                                lhsT_scale=k_plane[u][:, o, P * t : P * (t + 1)],
-                                rhs=q_codes[:, o, h * P : (h + 1) * P].bitcast(FP8X4),
-                                rhs_scale=q_plane[:, o, h * P : (h + 1) * P],
-                                start=(o == 0),
-                                stop=(o == DP - 1),
-                            )
-                for e in range(2):
-                    t = 2 * pair + e
-                    nc.scalar.activation(prob[u][:, t, :], bank[:, e, :], SIGMOID, bias=kb_col[u][:, t : t + 1])
+        def key_biases(u, got_tag):
+            kb_got = keep.tile([P, PASS], F32, name="kb_got%d" % u, tag=got_tag, align_bytes=64)
+            nc.vector.tensor_copy(kb_got[:], kb_win[:].indirect(lists(u)))
+            to_columns(kb_got[:], kb_col[u])
+
+        def token_scales(u, got_tag):
+            vs_got = keep.tile([P, PASS], F32, name="vs_got%d" % u, tag=got_tag, align_bytes=64)
+            nc.vector.tensor_copy(vs_got[:], vs_win[:].indirect(lists(u)))
+            to_columns(vs_got[:], vs_col[u])
+
+        def scores(u, h):
+            cols = slice(h * P, (h + 1) * P)
+            bank = score_ps.tile([P, PACK, P], F32, name="bank", tag="score")
+            for t in range(PACK):
+                for o in range(DP):
+                    nc.tensor.matmul_mx(
+                        out=bank[:, t, :],
+                        lhsT=k_codes[u][:, o, 2 * P * t : 2 * P * (t + 1)].bitcast(FP4X4),
+                        lhsT_scale=k_plane[:, o, PASS * u + P * t : PASS * u + P * (t + 1)],
+                        rhs=q_codes[:, o, cols].bitcast(FP8X4),
+                        rhs_scale=q_plane[:, o, cols],
+                        start=(o == 0),
+                        stop=(o == DP - 1),
+                    )
+            for t in range(PACK):
+                nc.scalar.activation(prob[u][:, t, cols], bank[:, t, :], SIGMOID, bias=kb_col[u][:, t : t + 1])
 
         def values():
             for u in range(SP):
@@ -165,24 +179,31 @@ def tile_attend_sigm_kb_gate_srtq256n1024t2048_kernel(
                 in_=w_bf[u][:, cols, :].rearrange("p q t -> p (q t)"),
             )
 
-        keys(0)
-        scores(0)
+        key_scales()
         values()
-        keys(1)
-        for u in range(SP):
-            nc.vector.tensor_copy(vs_got[u][:], vs_win[:].indirect(lists(u)))
-            to_columns(vs_got[u], vs_col[u])
-        scores(1)
-        nc.vector.quantize_mx(
-            out=v_codes[:].rearrange("p u e -> p (u e)").bitcast(FP8X4),
-            scales=v_plane[:].rearrange("p u e -> p (u e)"),
-            in_=v_bf[:].rearrange("p u e t -> p (u e t)"),
-        )
-        acc = [turn_ps.tile([P, DV], F32, name="acc%d" % h, tag="turn") for h in range(QH)]
-        result = [keep.tile([P, DV], F32, name="result%d" % h) for h in range(QH)]
+        key_biases(0, "kb_got0")
+        token_scales(0, "vs_got0")
+        key_words(0)
+        part_words(0)
+        key_words(1)
+        key_biases(1, "got0")
+        part_words(1)
+        token_scales(1, "got1")
         for u in range(SP):
             for h in range(QH):
-                weights(u, h)
+                scores(u, h)
+        acc = [turn_ps.tile([P, DV], F32, name="acc%d" % h, tag="turn") for h in range(QH)]
+        result = [keep.tile([P, DV], F32, name="result%d" % h) for h in range(QH)]
+        v_codes = keep.tile([P, SP, DV], U32, name="v_codes", tag="got0", align_bytes=64)
+        for u in range(SP):
+            weights(u, 0)
+            if u == 0:
+                nc.vector.quantize_mx(
+                    out=v_codes[:].rearrange("p u e -> p (u e)").bitcast(FP8X4),
+                    scales=v_plane[:].rearrange("p u e -> p (u e)"),
+                    in_=v_bf[:].rearrange("p u e t -> p (u e t)"),
+                )
+            weights(u, 1)
             for h in range(QH):
                 quantise_w(u, h)
                 nc.tensor.matmul_mx(

@@ -68,14 +68,13 @@ def tile_attend_sigm_kb_gate_srtq256n1024t2048_kernel(
                 q_scales[0][:, 4 * quad : 4 * quad + 4, :].rearrange("o f q -> f o q").bitcast(I32),
             )
         nc.sync.dma_start(v_raw[:, : T // 2], vT[:, : T // 2])
-        nc.sync.dma_start(v_raw[:, T // 2 :], vT[:, T // 2 :])
         nc.vector.memset(kb_win[:], 0.0)
         nc.sync.dma_start(kb_win[0:1, :], kb[0:1, :])
+        nc.sync.dma_start(v_raw[:, T // 2 :], vT[:, T // 2 :])
         nc.vector.memset(vs_win[:], 0.0)
         nc.sync.dma_start(vs_win[0:1, :], vs[0:1, :])
         k_rows = k_words[0].rearrange("p t b -> p (t b)").bitcast(I32)
         nc.sync.dma_start(kw_win[:, :REACH].bitcast(I32), k_rows[:, :REACH])
-        nc.sync.dma_start(q_codes[:].bitcast(I32), q_words[0].rearrange("o p q r -> p o (q r)").bitcast(I32))
         nc.sync.dma_start(kw_win[:, REACH:].bitcast(I32), k_rows[:, REACH:])
 
         nc.scalar.activation(gate[:], og_raw[:], SIGMOID)
@@ -114,6 +113,10 @@ def tile_attend_sigm_kb_gate_srtq256n1024t2048_kernel(
                         k_plane[32 * quad : 32 * quad + 4, o, :].bitcast(I32),
                         ks_laid[first : first + 16 : 4, :].bitcast(I32),
                     )
+                if o == 0:
+                    nc.sync.dma_start(
+                        q_codes[:].bitcast(I32), q_words[0].rearrange("o p q r -> p o (q r)").bitcast(I32)
+                    )
 
         def key_words(u):
             nc.vector.tensor_copy(kw_got[u][:].rearrange("g t p -> g p t"), kw_win[:, : (REACH, T)[u]].indirect(lists(u)))
@@ -124,15 +127,13 @@ def tile_attend_sigm_kb_gate_srtq256n1024t2048_kernel(
                 kw_got[u][:].rearrange("g t p -> g (t p)").bitcast(U16).rearrange("g (s o) -> g o s", o=DP),
             )
 
-        def key_biases(u, got_tag):
-            kb_got = keep.tile([P, PASS], F32, name="kb_got%d" % u, tag=got_tag, align_bytes=64)
-            nc.vector.tensor_copy(kb_got[:], kb_win[:].indirect(lists(u)))
-            to_columns(kb_got[:], kb_col[u])
+        def key_biases(u, got):
+            nc.vector.tensor_copy(got, kb_win[:].indirect(lists(u)))
+            to_columns(got, kb_col[u])
 
-        def token_scales(u, got_tag):
-            vs_got = keep.tile([P, PASS], F32, name="vs_got%d" % u, tag=got_tag, align_bytes=64)
-            nc.vector.tensor_copy(vs_got[:], vs_win[:].indirect(lists(u)))
-            to_columns(vs_got[:], vs_col[u])
+        def token_scales(u, got):
+            nc.vector.tensor_copy(got, vs_win[:].indirect(lists(u)))
+            to_columns(got, vs_col[u])
 
         def scores(u, h):
             cols = slice(h * P, (h + 1) * P)
@@ -181,20 +182,22 @@ def tile_attend_sigm_kb_gate_srtq256n1024t2048_kernel(
 
         key_scales()
         values()
-        key_biases(0, "kb_got0")
-        token_scales(0, "vs_got0")
+        early = keep.tile([P, 2, PASS], F32, name="early")
+        key_biases(0, early[:, 0, :])
+        token_scales(0, early[:, 1, :])
         key_words(0)
         part_words(0)
         key_words(1)
-        key_biases(1, "got0")
+        late = keep.tile([P, 2, PASS], F32, name="late", tag="got0", align_bytes=64)
+        key_biases(1, late[:, 0, :])
         part_words(1)
-        token_scales(1, "got1")
+        token_scales(1, late[:, 1, :])
         for u in range(SP):
             for h in range(QH):
                 scores(u, h)
         acc = [turn_ps.tile([P, DV], F32, name="acc%d" % h, tag="turn") for h in range(QH)]
         result = [keep.tile([P, DV], F32, name="result%d" % h) for h in range(QH)]
-        v_codes = keep.tile([P, SP, DV], U32, name="v_codes", tag="got0", align_bytes=64)
+        v_codes = keep.tile([P, SP, DV], U32, name="v_codes", tag="got1", align_bytes=64)
         for u in range(SP):
             weights(u, 0)
             if u == 0:

@@ -26,6 +26,7 @@ SP = N // PASS
 QH = NQ // P
 COLS = PASS // 16
 REACH = T - N + PASS
+HALF = P // 2
 
 
 def tile_attend_sigm_kb_gate_srtq256n1024t2048_kernel(
@@ -34,15 +35,16 @@ def tile_attend_sigm_kb_gate_srtq256n1024t2048_kernel(
     nc = tc.nc
     with ExitStack() as ctx:
         keep = ctx.enter_context(tc.tile_pool(name="keep", bufs=1))
-        score_ps = ctx.enter_context(tc.psum_pool(name="score_ps", bufs=2))
+        score_ps = ctx.enter_context(tc.psum_pool(name="score_ps", bufs=3))
         turn_ps = ctx.enter_context(tc.psum_pool(name="turn_ps", bufs=3))
 
         offsets = keep.tile([P, N // 16], U16, name="offsets")
         kw_win = keep.tile([P, T], U32, name="kw_win")
         ks_win = keep.tile([P, T], U8, name="ks_win")
         kb_win = keep.tile([P, T], F32, name="kb_win")
-        vs_win = keep.tile([P, T], F32, name="vs_win")
-        v_raw = keep.tile([P, T], F32, name="v_raw")
+        vs_win = keep.tile([P, T], F32, name="vs_win", tag="scales", align_bytes=64)
+        v_head = keep.tile([P, REACH], F32, name="v_head")
+        v_tail = keep.tile([P, T - REACH], F32, name="v_tail")
         v_win = keep.tile([P, T], BF16, name="v_win")
         q_codes = keep.tile([P, DP, NQ], U32, name="q_codes", align_bytes=64)
         q_plane = keep.tile([P, DP, NQ], U8, name="q_plane", align_bytes=64)
@@ -51,40 +53,44 @@ def tile_attend_sigm_kb_gate_srtq256n1024t2048_kernel(
         ident = keep.tile([P, P], F32, name="ident")
 
         ks_got = keep.tile([P, N], U8, name="ks_got")
-        ks_laid = keep.tile([P, N], U8, name="ks_laid")
-        k_plane = keep.tile([P, DP, N], U8, name="k_plane", align_bytes=64)
+        k_plane = [keep.tile([P, N], U8, name="k_plane%d" % o, align_bytes=64) for o in range(DP)]
 
         nc.gpsimd.memset(q_plane[:].bitcast(I32), 0)
         make_identity(nc, ident[:])
         nc.sync.dma_start(offsets[:], offs)
-        nc.sync.dma_start(
-            ks_win[:].bitcast(I32),
-            k_scales.rearrange("o f t -> (o f) t").bitcast(I32).unsqueeze(1).to_broadcast([32, 4, T // 4]),
-        )
+        ks_rows = k_scales.rearrange("o f t -> (o f) t").bitcast(I32)
+        nc.sync.dma_start(ks_win[0:32, :].bitcast(I32), ks_rows)
+        for quad in range(1, 4):
+            nc.sync.dma_start(
+                ks_win[32 * quad : 32 * quad + 32, :].bitcast(I32),
+                ks_rows[4 * quad : 4 * quad + 16, :].unsqueeze(0).to_broadcast([2, 16, T // 4]),
+            )
         nc.sync.dma_start(og_raw[:], og[0].rearrange("(h p) e -> p h e", p=P))
+        nc.sync.dma_start(v_head[:], vT[:, :REACH])
+        k_rows = k_words[0].rearrange("p t b -> p (t b)").bitcast(I32)
+        nc.vector.memset(kb_win[:], 0.0)
+        nc.sync.dma_start(kb_win[0:1, :], kb[0:1, :])
+        nc.vector.memset(vs_win[:], 0.0)
+        nc.sync.dma_start(vs_win[0:1, :], vs[0:1, :])
+        nc.sync.dma_start(kw_win[:, :REACH].bitcast(I32), k_rows[:, :REACH])
         for quad in range(4):
             nc.sync.dma_start(
                 q_plane[32 * quad : 32 * quad + 4, :, :].bitcast(I32),
                 q_scales[0][:, 4 * quad : 4 * quad + 4, :].rearrange("o f q -> f o q").bitcast(I32),
             )
-        nc.sync.dma_start(v_raw[:, : T // 2], vT[:, : T // 2])
-        nc.vector.memset(kb_win[:], 0.0)
-        nc.sync.dma_start(kb_win[0:1, :], kb[0:1, :])
-        nc.sync.dma_start(v_raw[:, T // 2 :], vT[:, T // 2 :])
-        nc.vector.memset(vs_win[:], 0.0)
-        nc.sync.dma_start(vs_win[0:1, :], vs[0:1, :])
-        k_rows = k_words[0].rearrange("p t b -> p (t b)").bitcast(I32)
-        nc.sync.dma_start(kw_win[:, :REACH].bitcast(I32), k_rows[:, :REACH])
-        nc.sync.dma_start(kw_win[:, REACH:].bitcast(I32), k_rows[:, REACH:])
+        nc.sync.dma_start(v_tail[:], vT[:, REACH:])
+        nc.sync.dma_start(q_codes[:].bitcast(I32), q_words[0].rearrange("o p q r -> p o (q r)").bitcast(I32))
 
         nc.scalar.activation(gate[:], og_raw[:], SIGMOID)
-        nc.scalar.copy(v_win[:, : T // 2], v_raw[:, : T // 2])
-        nc.scalar.copy(v_win[:, T // 2 :], v_raw[:, T // 2 :])
+        nc.scalar.copy(v_win[:, :REACH], v_head[:])
 
         def lists(u):
             return offsets[:, u * COLS : (u + 1) * COLS]
 
-        kw_got = [keep.tile([P, PACK, P], U32, name="kw_got%d" % u, tag="got%d" % u, align_bytes=64) for u in range(SP)]
+        kw_got = [
+            [keep.tile([P, PACK, HALF], U32, name="kw_got%d%d" % (u, j), tag="got%d%d" % (u, j)) for j in range(2)]
+            for u in range(SP)
+        ]
         k_codes = [keep.tile([P, DP, 2 * PASS], U8, name="k_codes%d" % u, align_bytes=64) for u in range(SP)]
         kb_col = [keep.tile([P, PACK], F32, name="kb_col%d" % u) for u in range(SP)]
         vs_col = [keep.tile([P, PACK], F32, name="vs_col%d" % u) for u in range(SP)]
@@ -92,7 +98,7 @@ def tile_attend_sigm_kb_gate_srtq256n1024t2048_kernel(
         w_bf = [keep.tile([P, NQ, PACK], BF16, name="w_bf%d" % u, align_bytes=64) for u in range(SP)]
         w_codes = [keep.tile([P, NQ], U32, name="w_codes%d" % u, align_bytes=64) for u in range(SP)]
         w_plane = [keep.tile([P, NQ], U8, name="w_plane%d" % u, align_bytes=64) for u in range(SP)]
-        v_got = keep.tile([P, SP, 2, P, 2], BF16, name="v_got")
+        v_got = [keep.tile([P, 2, P, 2], BF16, name="v_got%d" % u) for u in range(SP)]
         v_bf = keep.tile([P, SP, DV, PACK], BF16, name="v_bf", align_bytes=64)
         v_plane = keep.tile([P, SP, DV], U8, name="v_plane", align_bytes=64)
 
@@ -100,32 +106,39 @@ def tile_attend_sigm_kb_gate_srtq256n1024t2048_kernel(
             nc.sync.dma_start(col[:], got[0:1, :].rearrange("o (p t) -> o p t", t=PACK))
 
         def key_scales():
-            nc.vector.tensor_copy(ks_got[:], ks_win[:].indirect(offsets[:]))
-            nc.vector.memset(k_plane[:].bitcast(I32), 0)
-            nc.vector.tensor_copy(
-                ks_laid[:].rearrange("g (u t p) -> g u t p", u=SP, t=PACK),
-                ks_got[:].rearrange("g (u p t) -> g u t p", u=SP, t=PACK),
-            )
-            for o in range(DP):
-                for quad in range(4):
-                    first = 64 * o + 16 * quad
-                    nc.sync.dma_start(
-                        k_plane[32 * quad : 32 * quad + 4, o, :].bitcast(I32),
-                        ks_laid[first : first + 16 : 4, :].bitcast(I32),
-                    )
-                if o == 0:
-                    nc.sync.dma_start(
-                        q_codes[:].bitcast(I32), q_words[0].rearrange("o p q r -> p o (q r)").bitcast(I32)
-                    )
+            for u in range(SP):
+                nc.vector.tensor_copy(ks_got[:, u * PASS : (u + 1) * PASS], ks_win[:].indirect(lists(u)))
+            for u in range(SP):
+                nc.vector.tensor_copy(
+                    k_plane[0][:, u * PASS : (u + 1) * PASS].rearrange("g (t p) -> g t p", t=PACK),
+                    ks_got[:, u * PASS : (u + 1) * PASS].rearrange("g (p t) -> g t p", t=PACK),
+                )
+            for first, count, source in ((0, 64, 44), (64, 32, 24), (96, 32, 28)):
+                nc.sync.dma_start(
+                    k_plane[1][first : first + count, :].bitcast(I32),
+                    k_plane[0][source : source + count, :].bitcast(I32),
+                )
+            nc.sync.dma_start(kw_win[:, REACH:].bitcast(I32), k_rows[:, REACH:])
 
         def key_words(u):
-            nc.vector.tensor_copy(kw_got[u][:].rearrange("g t p -> g p t"), kw_win[:, : (REACH, T)[u]].indirect(lists(u)))
+            for j in range(2):
+                first = u * COLS + j * COLS // 2
+                nc.vector.tensor_copy(
+                    kw_got[u][j][:].rearrange("g t p -> g p t"),
+                    kw_win[:, : (REACH, T)[u]].indirect(offsets[:, first : first + COLS // 2]),
+                )
 
         def part_words(u):
-            nc.vector.tensor_copy(
-                k_codes[u][:].bitcast(U16),
-                kw_got[u][:].rearrange("g t p -> g (t p)").bitcast(U16).rearrange("g (s o) -> g o s", o=DP),
-            )
+            for j in range(2):
+                nc.vector.tensor_copy(
+                    k_codes[u][:].bitcast(U16).rearrange("g o (t p) -> g o t p", t=PACK)[
+                        :, :, :, j * HALF : (j + 1) * HALF
+                    ],
+                    kw_got[u][j][:]
+                    .rearrange("g t p -> g (t p)")
+                    .bitcast(U16)
+                    .rearrange("g (t p o) -> g o t p", t=PACK, o=DP),
+                )
 
         def key_biases(u, got):
             nc.vector.tensor_copy(got, kb_win[:].indirect(lists(u)))
@@ -138,30 +151,29 @@ def tile_attend_sigm_kb_gate_srtq256n1024t2048_kernel(
         def scores(u, h):
             cols = slice(h * P, (h + 1) * P)
             bank = score_ps.tile([P, PACK, P], F32, name="bank", tag="score")
-            for t in range(PACK):
-                for o in range(DP):
+            for o in range(DP):
+                for t in range(PACK):
                     nc.tensor.matmul_mx(
                         out=bank[:, t, :],
                         lhsT=k_codes[u][:, o, 2 * P * t : 2 * P * (t + 1)].bitcast(FP4X4),
-                        lhsT_scale=k_plane[:, o, PASS * u + P * t : PASS * u + P * (t + 1)],
+                        lhsT_scale=k_plane[o][:, PASS * u + P * t : PASS * u + P * (t + 1)],
                         rhs=q_codes[:, o, cols].bitcast(FP8X4),
                         rhs_scale=q_plane[:, o, cols],
-                        start=(o == 0),
-                        stop=(o == DP - 1),
+                        start=(o == 0 and t == 0),
+                        stop=(o == DP - 1 and t == PACK - 1),
                     )
             for t in range(PACK):
                 nc.scalar.activation(prob[u][:, t, cols], bank[:, t, :], SIGMOID, bias=kb_col[u][:, t : t + 1])
 
-        def values():
-            for u in range(SP):
-                nc.scalar.activation(v_got[:, u].rearrange("e h p r -> e p h r"), v_win[:].indirect(lists(u)), COPY)
-            turned = turn_ps.tile([P, SP, 2, DV], F32, name="turned_v", tag="turn")
-            for u in range(SP):
-                for h in range(2):
-                    nc.tensor.transpose(
-                        turned[:, u, h, :], v_got[:, u, h].rearrange("e p r -> e (p r)").bitcast(F32), ident[:]
-                    )
-            nc.scalar.copy(v_bf[:].bitcast(F32), turned[:].rearrange("p u h e -> p u e h"))
+        def gather_values(u):
+            nc.scalar.activation(
+                v_got[u][:].rearrange("e h p r -> e p h r"), v_win[:, : (REACH, T)[u]].indirect(lists(u)), COPY
+            )
+
+        def turn_values(u, turned):
+            for h in range(2):
+                nc.tensor.transpose(turned[:, h, :], v_got[u][:, h].rearrange("e p r -> e (p r)").bitcast(F32), ident[:])
+            nc.scalar.copy(v_bf[:, u].bitcast(F32), turned[:, 0:2, :].rearrange("p h e -> p e h"))
 
         def weights(u, h):
             cols = slice(h * P, (h + 1) * P)
@@ -181,23 +193,29 @@ def tile_attend_sigm_kb_gate_srtq256n1024t2048_kernel(
             )
 
         key_scales()
-        values()
+        gather_values(0)
+        nc.scalar.copy(v_win[:, REACH:], v_tail[:])
+        gather_values(1)
+        turn_values(0, turn_ps.tile([P, PACK, DV], F32, name="turned0", tag="turn"))
         early = keep.tile([P, 2, PASS], F32, name="early")
         key_biases(0, early[:, 0, :])
         token_scales(0, early[:, 1, :])
         key_words(0)
         part_words(0)
+        late_kb = keep.tile([P, PASS], F32, name="late_kb", tag="got00")
+        key_biases(1, late_kb[:])
         key_words(1)
-        late = keep.tile([P, 2, PASS], F32, name="late", tag="got0", align_bytes=64)
-        key_biases(1, late[:, 0, :])
         part_words(1)
-        token_scales(1, late[:, 1, :])
-        for u in range(SP):
-            for h in range(QH):
-                scores(u, h)
+        late_vs = keep.tile([P, PASS], F32, name="late_vs", tag="got10")
+        token_scales(1, late_vs[:])
+        scores(0, 0)
+        scores(0, 1)
+        scores(1, 0)
+        turn_values(1, score_ps.tile([P, PACK, P], F32, name="turned1", tag="score"))
+        scores(1, 1)
         acc = [turn_ps.tile([P, DV], F32, name="acc%d" % h, tag="turn") for h in range(QH)]
         result = [keep.tile([P, DV], F32, name="result%d" % h) for h in range(QH)]
-        v_codes = keep.tile([P, SP, DV], U32, name="v_codes", tag="got1", align_bytes=64)
+        v_codes = keep.tile([P, SP, DV], U32, name="v_codes", tag="scales", align_bytes=64)
         for u in range(SP):
             weights(u, 0)
             if u == 0:

@@ -48,22 +48,21 @@ def tile_attend_sigm_kb_gate_srtq256n1024t2048_kernel(
         v_win = keep.tile([P, T], BF16, name="v_win")
         q_codes = keep.tile([P, DP, NQ], U32, name="q_codes", align_bytes=64)
         q_plane = keep.tile([P, DP, NQ], U8, name="q_plane", align_bytes=64)
-        og_raw = keep.tile([P, QH, DV], F32, name="og_raw")
+        og_raw = keep.tile([P, QH, DV], F32, name="og_raw", tag="og")
         gate = keep.tile([P, QH, DV], F32, name="gate")
-        ident = keep.tile([P, P], F32, name="ident")
 
         ks_got = keep.tile([P, N], U8, name="ks_got")
         k_plane = [keep.tile([P, N], U8, name="k_plane%d" % o, align_bytes=64) for o in range(DP)]
 
+        nc.gpsimd.memset(ks_win[:].bitcast(I32), 0)
         nc.gpsimd.memset(q_plane[:].bitcast(I32), 0)
-        make_identity(nc, ident[:])
         nc.sync.dma_start(offsets[:], offs)
         ks_rows = k_scales.rearrange("o f t -> (o f) t").bitcast(I32)
-        nc.sync.dma_start(ks_win[0:32, :].bitcast(I32), ks_rows)
+        nc.scalar.dma_start(ks_win[0:32, :].bitcast(I32), ks_rows)
         for quad in range(1, 4):
-            nc.sync.dma_start(
-                ks_win[32 * quad : 32 * quad + 32, :].bitcast(I32),
-                ks_rows[4 * quad : 4 * quad + 16, :].unsqueeze(0).to_broadcast([2, 16, T // 4]),
+            nc.scalar.dma_start(
+                ks_win[32 * quad : 32 * quad + 16, :].bitcast(I32),
+                ks_rows[4 * quad : 4 * quad + 16, :],
             )
         nc.sync.dma_start(og_raw[:], og[0].rearrange("(h p) e -> p h e", p=P))
         nc.sync.dma_start(v_head[:], vT[:, :REACH])
@@ -82,6 +81,8 @@ def tile_attend_sigm_kb_gate_srtq256n1024t2048_kernel(
         nc.sync.dma_start(q_codes[:].bitcast(I32), q_words[0].rearrange("o p q r -> p o (q r)").bitcast(I32))
 
         nc.scalar.activation(gate[:], og_raw[:], SIGMOID)
+        ident = keep.tile([P, P], BF16, name="ident", tag="og")
+        make_identity(nc, ident[:])
         nc.scalar.copy(v_win[:, :REACH], v_head[:])
 
         def lists(u):
@@ -98,20 +99,23 @@ def tile_attend_sigm_kb_gate_srtq256n1024t2048_kernel(
         w_bf = [keep.tile([P, NQ, PACK], BF16, name="w_bf%d" % u, align_bytes=64) for u in range(SP)]
         w_codes = [keep.tile([P, NQ], U32, name="w_codes%d" % u, align_bytes=64) for u in range(SP)]
         w_plane = [keep.tile([P, NQ], U8, name="w_plane%d" % u, align_bytes=64) for u in range(SP)]
-        v_got = [keep.tile([P, 2, P, 2], BF16, name="v_got%d" % u) for u in range(SP)]
+        v_got = [keep.tile([P, PACK, P], BF16, name="v_got%d" % u) for u in range(SP)]
         v_bf = keep.tile([P, SP, DV, PACK], BF16, name="v_bf", align_bytes=64)
         v_plane = keep.tile([P, SP, DV], U8, name="v_plane", align_bytes=64)
 
         def to_columns(got, col):
             nc.sync.dma_start(col[:], got[0:1, :].rearrange("o (p t) -> o p t", t=PACK))
 
+        def by_column(got):
+            return got.bitcast(U32).rearrange("g (m i t) -> g m t i", i=4, t=PACK)
+
         def key_scales():
             for u in range(SP):
                 nc.vector.tensor_copy(ks_got[:, u * PASS : (u + 1) * PASS], ks_win[:].indirect(lists(u)))
             for u in range(SP):
                 nc.vector.tensor_copy(
-                    k_plane[0][:, u * PASS : (u + 1) * PASS].rearrange("g (t p) -> g t p", t=PACK),
-                    ks_got[:, u * PASS : (u + 1) * PASS].rearrange("g (p t) -> g t p", t=PACK),
+                    k_plane[0][:, u * PASS : (u + 1) * PASS].bitcast(I32).rearrange("g (t m) -> g t m", t=PACK),
+                    ks_got[:, u * PASS : (u + 1) * PASS].bitcast(I32).rearrange("g (m t) -> g t m", t=PACK),
                 )
             for first, count, source in ((0, 64, 44), (64, 32, 24), (96, 32, 28)):
                 nc.sync.dma_start(
@@ -124,7 +128,7 @@ def tile_attend_sigm_kb_gate_srtq256n1024t2048_kernel(
             for j in range(2):
                 first = u * COLS + j * COLS // 2
                 nc.vector.tensor_copy(
-                    kw_got[u][j][:].rearrange("g t p -> g p t"),
+                    kw_got[u][j][:].rearrange("g t (m i) -> g m t i", i=4),
                     kw_win[:, : (REACH, T)[u]].indirect(offsets[:, first : first + COLS // 2]),
                 )
 
@@ -141,11 +145,11 @@ def tile_attend_sigm_kb_gate_srtq256n1024t2048_kernel(
                 )
 
         def key_biases(u, got):
-            nc.vector.tensor_copy(got, kb_win[:].indirect(lists(u)))
+            nc.vector.tensor_copy(by_column(got), kb_win[:].bitcast(U32).indirect(lists(u)))
             to_columns(got, kb_col[u])
 
         def token_scales(u, got):
-            nc.vector.tensor_copy(got, vs_win[:].indirect(lists(u)))
+            nc.vector.tensor_copy(by_column(got), vs_win[:].bitcast(U32).indirect(lists(u)))
             to_columns(got, vs_col[u])
 
         def scores(u, h):
@@ -167,13 +171,15 @@ def tile_attend_sigm_kb_gate_srtq256n1024t2048_kernel(
 
         def gather_values(u):
             nc.scalar.activation(
-                v_got[u][:].rearrange("e h p r -> e p h r"), v_win[:, : (REACH, T)[u]].indirect(lists(u)), COPY
+                v_got[u][:].rearrange("e t (m i) -> e m t i", i=4), v_win[:, : (REACH, T)[u]].indirect(lists(u)), COPY
             )
 
         def turn_values(u, turned):
-            for h in range(2):
-                nc.tensor.transpose(turned[:, h, :], v_got[u][:, h].rearrange("e p r -> e (p r)").bitcast(F32), ident[:])
-            nc.scalar.copy(v_bf[:, u].bitcast(F32), turned[:, 0:2, :].rearrange("p h e -> p e h"))
+            for t in range(PACK):
+                nc.tensor.transpose(turned[:, t, :], v_got[u][:, t, :], ident[:])
+            nc.scalar.copy(
+                v_bf[:, u].rearrange("p (c i) t -> p c t i", i=4), turned[:].rearrange("p t (c i) -> p c t i", i=4)
+            )
 
         def weights(u, h):
             cols = slice(h * P, (h + 1) * P)
@@ -196,7 +202,7 @@ def tile_attend_sigm_kb_gate_srtq256n1024t2048_kernel(
         gather_values(0)
         nc.scalar.copy(v_win[:, REACH:], v_tail[:])
         gather_values(1)
-        turn_values(0, turn_ps.tile([P, PACK, DV], F32, name="turned0", tag="turn"))
+        turn_values(0, turn_ps.tile([P, PACK, DV], BF16, name="turned0", tag="turn"))
         early = keep.tile([P, 2, PASS], F32, name="early")
         key_biases(0, early[:, 0, :])
         token_scales(0, early[:, 1, :])
@@ -211,7 +217,7 @@ def tile_attend_sigm_kb_gate_srtq256n1024t2048_kernel(
         scores(0, 0)
         scores(0, 1)
         scores(1, 0)
-        turn_values(1, score_ps.tile([P, PACK, P], F32, name="turned1", tag="score"))
+        turn_values(1, score_ps.tile([P, PACK, P], BF16, name="turned1", tag="score"))
         scores(1, 1)
         acc = [turn_ps.tile([P, DV], F32, name="acc%d" % h, tag="turn") for h in range(QH)]
         result = [keep.tile([P, DV], F32, name="result%d" % h) for h in range(QH)]

@@ -54,15 +54,18 @@ def tile_attend_sigm_kb_gate_srtq256n1024t2048_kernel(
         ks_got = keep.tile([P, N], U8, name="ks_got")
         k_plane = [keep.tile([P, N], U8, name="k_plane%d" % o, align_bytes=64) for o in range(DP)]
 
-        nc.gpsimd.memset(ks_win[:].bitcast(I32), 0)
+        nc.gpsimd.memset(ks_win[64:128, :].bitcast(I32), 0)
         nc.gpsimd.memset(q_plane[:].bitcast(I32), 0)
         nc.sync.dma_start(offsets[:], offs)
         ks_rows = k_scales.rearrange("o f t -> (o f) t").bitcast(I32)
-        nc.scalar.dma_start(ks_win[0:32, :].bitcast(I32), ks_rows)
-        for quad in range(1, 4):
-            nc.scalar.dma_start(
-                ks_win[32 * quad : 32 * quad + 16, :].bitcast(I32),
-                ks_rows[4 * quad : 4 * quad + 16, :],
+        nc.sync.dma_start(ks_win[0:32, :].bitcast(I32), ks_rows)
+        nc.sync.dma_start(
+            ks_win[32:64, :].bitcast(I32), ks_rows[4:8, :].unsqueeze(0).to_broadcast([8, 4, T // 4])
+        )
+        for quad in range(2, 4):
+            nc.sync.dma_start(
+                ks_win[32 * quad : 32 * quad + 4, :].bitcast(I32),
+                ks_rows[4 * quad : 4 * quad + 4, :],
             )
         nc.sync.dma_start(og_raw[:], og[0].rearrange("(h p) e -> p h e", p=P))
         nc.sync.dma_start(v_head[:], vT[:, :REACH])
@@ -77,8 +80,8 @@ def tile_attend_sigm_kb_gate_srtq256n1024t2048_kernel(
                 q_plane[32 * quad : 32 * quad + 4, :, :].bitcast(I32),
                 q_scales[0][:, 4 * quad : 4 * quad + 4, :].rearrange("o f q -> f o q").bitcast(I32),
             )
-        nc.sync.dma_start(v_tail[:], vT[:, REACH:])
         nc.sync.dma_start(q_codes[:].bitcast(I32), q_words[0].rearrange("o p q r -> p o (q r)").bitcast(I32))
+        nc.sync.dma_start(v_tail[:], vT[:, REACH:])
 
         nc.scalar.activation(gate[:], og_raw[:], SIGMOID)
         ident = keep.tile([P, P], BF16, name="ident", tag="og")
@@ -117,10 +120,10 @@ def tile_attend_sigm_kb_gate_srtq256n1024t2048_kernel(
                     k_plane[0][:, u * PASS : (u + 1) * PASS].bitcast(I32).rearrange("g (t m) -> g t m", t=PACK),
                     ks_got[:, u * PASS : (u + 1) * PASS].bitcast(I32).rearrange("g (m t) -> g t m", t=PACK),
                 )
-            for first, count, source in ((0, 64, 44), (64, 32, 24), (96, 32, 28)):
+            for quad in range(4):
                 nc.sync.dma_start(
-                    k_plane[1][first : first + count, :].bitcast(I32),
-                    k_plane[0][source : source + count, :].bitcast(I32),
+                    k_plane[1][32 * quad : 32 * quad + 32, :].bitcast(I32),
+                    k_plane[0][16 + 4 * quad : 48 + 4 * quad, :].bitcast(I32),
                 )
             nc.sync.dma_start(kw_win[:, REACH:].bitcast(I32), k_rows[:, REACH:])
 

@@ -26,7 +26,8 @@ SP = N // PASS
 QH = NQ // P
 COLS = PASS // 16
 REACH = T - N + PASS
-HALF = P // 2
+ROW = P - 1
+KS0 = 96
 
 
 def tile_attend_sigm_kb_gate_srtq256n1024t2048_kernel(
@@ -35,160 +36,120 @@ def tile_attend_sigm_kb_gate_srtq256n1024t2048_kernel(
     nc = tc.nc
     with ExitStack() as ctx:
         keep = ctx.enter_context(tc.tile_pool(name="keep", bufs=1))
-        score_ps = ctx.enter_context(tc.psum_pool(name="score_ps", bufs=3))
-        turn_ps = ctx.enter_context(tc.psum_pool(name="turn_ps", bufs=3))
+        psum = ctx.enter_context(tc.psum_pool(name="psum", bufs=1))
 
         offsets = keep.tile([P, N // 16], U16, name="offsets")
         kw_win = keep.tile([P, T], U32, name="kw_win")
         ks_win = keep.tile([P, T], U8, name="ks_win")
         kb_win = keep.tile([P, T], F32, name="kb_win")
-        vs_win = keep.tile([P, T], F32, name="vs_win", tag="scales", align_bytes=64)
-        v_head = keep.tile([P, REACH], F32, name="v_head")
-        v_tail = keep.tile([P, T - REACH], F32, name="v_tail")
-        v_win = keep.tile([P, T], BF16, name="v_win")
+        vs_win = keep.tile([P, T], F32, name="vs_win")
         q_codes = keep.tile([P, DP, NQ], U32, name="q_codes", align_bytes=64)
         q_plane = keep.tile([P, DP, NQ], U8, name="q_plane", align_bytes=64)
+        k_plane = keep.tile([P, DP, N], U8, name="k_plane", align_bytes=64)
         og_raw = keep.tile([P, QH, DV], F32, name="og_raw", tag="og")
         gate = keep.tile([P, QH, DV], F32, name="gate")
+        ident = keep.tile([P, P], F32, name="ident")
 
-        ks_got = keep.tile([P, N], U8, name="ks_got")
-        k_plane = [keep.tile([P, N], U8, name="k_plane%d" % o, align_bytes=64) for o in range(DP)]
-
-        nc.gpsimd.memset(ks_win[64:128, :].bitcast(I32), 0)
         nc.gpsimd.memset(q_plane[:].bitcast(I32), 0)
-        nc.sync.dma_start(offsets[:], offs)
-        ks_rows = k_scales.rearrange("o f t -> (o f) t").bitcast(I32)
-        nc.sync.dma_start(ks_win[0:32, :].bitcast(I32), ks_rows)
-        nc.sync.dma_start(
-            ks_win[32:64, :].bitcast(I32), ks_rows[4:8, :].unsqueeze(0).to_broadcast([8, 4, T // 4])
-        )
-        for quad in range(2, 4):
-            nc.sync.dma_start(
-                ks_win[32 * quad : 32 * quad + 4, :].bitcast(I32),
-                ks_rows[4 * quad : 4 * quad + 4, :],
-            )
-        nc.sync.dma_start(og_raw[:], og[0].rearrange("(h p) e -> p h e", p=P))
-        nc.sync.dma_start(v_head[:], vT[:, :REACH])
+        nc.gpsimd.memset(k_plane[:].bitcast(I32), 0)
+        make_identity(nc, ident[:])
+        nc.vector.memset(ks_win[:KS0, :].bitcast(I32), 0)
+        nc.vector.memset(kb_win[:ROW, :], 0.0)
+        nc.vector.memset(vs_win[:ROW, :], 0.0)
+
         k_rows = k_words[0].rearrange("p t b -> p (t b)").bitcast(I32)
-        nc.vector.memset(kb_win[:], 0.0)
-        nc.sync.dma_start(kb_win[0:1, :], kb[0:1, :])
-        nc.vector.memset(vs_win[:], 0.0)
-        nc.sync.dma_start(vs_win[0:1, :], vs[0:1, :])
+        nc.sync.dma_start(offsets[:], offs)
+        nc.sync.dma_start(ks_win[KS0:, :].bitcast(I32), k_scales.rearrange("o f t -> f o t").bitcast(I32))
+        nc.sync.dma_start(og_raw[:], og[0].rearrange("(h p) e -> p h e", p=P))
+        nc.sync.dma_start(kb_win[ROW:, :], kb[0:1, :])
+        nc.sync.dma_start(vs_win[ROW:, :], vs[0:1, :])
+        nc.sync.dma_start(q_codes[:].bitcast(I32), q_words[0].rearrange("o p q r -> p o (q r)").bitcast(I32))
         nc.sync.dma_start(kw_win[:, :REACH].bitcast(I32), k_rows[:, :REACH])
         for quad in range(4):
             nc.sync.dma_start(
                 q_plane[32 * quad : 32 * quad + 4, :, :].bitcast(I32),
                 q_scales[0][:, 4 * quad : 4 * quad + 4, :].rearrange("o f q -> f o q").bitcast(I32),
             )
-        nc.sync.dma_start(q_codes[:].bitcast(I32), q_words[0].rearrange("o p q r -> p o (q r)").bitcast(I32))
-        nc.sync.dma_start(v_tail[:], vT[:, REACH:])
+        nc.sync.dma_start(kw_win[:, REACH:].bitcast(I32), k_rows[:, REACH:])
 
         nc.scalar.activation(gate[:], og_raw[:], SIGMOID)
-        ident = keep.tile([P, P], BF16, name="ident", tag="og")
-        make_identity(nc, ident[:])
-        nc.scalar.copy(v_win[:, :REACH], v_head[:])
+        v_win = keep.tile([P, T], F32, name="v_win", tag="og")
+        nc.scalar.dma_start(v_win[:], vT)
 
         def lists(u):
             return offsets[:, u * COLS : (u + 1) * COLS]
 
-        kw_got = [
-            [keep.tile([P, PACK, HALF], U32, name="kw_got%d%d" % (u, j), tag="got%d%d" % (u, j)) for j in range(2)]
-            for u in range(SP)
-        ]
+        ks_got = keep.tile([P, N], U8, name="ks_got")
+        kw_got = [keep.tile([P, PACK, P], U32, name="kw_got%d" % u) for u in range(SP)]
         k_codes = [keep.tile([P, DP, 2 * PASS], U8, name="k_codes%d" % u, align_bytes=64) for u in range(SP)]
+        kb_got = [keep.tile([P, PASS], F32, name="kb_got%d" % u) for u in range(SP)]
+        vs_got = [keep.tile([P, PASS], F32, name="vs_got%d" % u) for u in range(SP)]
         kb_col = [keep.tile([P, PACK], F32, name="kb_col%d" % u) for u in range(SP)]
         vs_col = [keep.tile([P, PACK], F32, name="vs_col%d" % u) for u in range(SP)]
-        prob = [keep.tile([P, PACK, NQ], F32, name="prob%d" % u) for u in range(SP)]
-        w_bf = [keep.tile([P, NQ, PACK], BF16, name="w_bf%d" % u, align_bytes=64) for u in range(SP)]
+        prob = [[keep.tile([P, PACK, P], F32, name="prob%d%d" % (u, h)) for h in range(QH)] for u in range(SP)]
+        w_bf = [[keep.tile([P, P, PACK], BF16, name="w_bf%d%d" % (u, h), align_bytes=64) for h in range(QH)] for u in range(SP)]
         w_codes = [keep.tile([P, NQ], U32, name="w_codes%d" % u, align_bytes=64) for u in range(SP)]
         w_plane = [keep.tile([P, NQ], U8, name="w_plane%d" % u, align_bytes=64) for u in range(SP)]
-        v_got = [keep.tile([P, PACK, P], BF16, name="v_got%d" % u) for u in range(SP)]
+        v_got = [keep.tile([P, PASS], BF16, name="v_got%d" % u) for u in range(SP)]
         v_bf = keep.tile([P, SP, DV, PACK], BF16, name="v_bf", align_bytes=64)
+        v_codes = keep.tile([P, SP, DV], U32, name="v_codes", align_bytes=64)
         v_plane = keep.tile([P, SP, DV], U8, name="v_plane", align_bytes=64)
+        result = [keep.tile([P, DV], F32, name="result%d" % h) for h in range(QH)]
 
-        def to_columns(got, col):
-            nc.sync.dma_start(col[:], got[0:1, :].rearrange("o (p t) -> o p t", t=PACK))
-
-        def by_column(got):
-            return got.bitcast(U32).rearrange("g (m i t) -> g m t i", i=4, t=PACK)
+        def row_gather(win, got, col, u):
+            nc.scalar.activation(got[:], win[:].indirect(lists(u)), COPY)
+            nc.sync.dma_start(col[:], got[ROW:, :].rearrange("o (p t) -> o p t", t=PACK))
 
         def key_scales():
-            for u in range(SP):
-                nc.vector.tensor_copy(ks_got[:, u * PASS : (u + 1) * PASS], ks_win[:].indirect(lists(u)))
-            for u in range(SP):
-                nc.vector.tensor_copy(
-                    k_plane[0][:, u * PASS : (u + 1) * PASS].bitcast(I32).rearrange("g (t m) -> g t m", t=PACK),
-                    ks_got[:, u * PASS : (u + 1) * PASS].bitcast(I32).rearrange("g (m t) -> g t m", t=PACK),
-                )
+            nc.vector.tensor_copy(
+                ks_got[:].rearrange("g (u t p) -> g u p t", u=SP, t=PACK), ks_win[:].indirect(offsets[:])
+            )
             for quad in range(4):
                 nc.sync.dma_start(
-                    k_plane[1][32 * quad : 32 * quad + 32, :].bitcast(I32),
-                    k_plane[0][16 + 4 * quad : 48 + 4 * quad, :].bitcast(I32),
-                )
-            nc.sync.dma_start(kw_win[:, REACH:].bitcast(I32), k_rows[:, REACH:])
-
-        def key_words(u):
-            for j in range(2):
-                first = u * COLS + j * COLS // 2
-                nc.vector.tensor_copy(
-                    kw_got[u][j][:].rearrange("g t (m i) -> g m t i", i=4),
-                    kw_win[:, : (REACH, T)[u]].indirect(offsets[:, first : first + COLS // 2]),
+                    k_plane[32 * quad : 32 * quad + 4, :, :].bitcast(I32),
+                    ks_got[KS0 + 8 * quad : KS0 + 8 * quad + 8, :].bitcast(I32),
                 )
 
-        def part_words(u):
-            for j in range(2):
-                nc.vector.tensor_copy(
-                    k_codes[u][:].bitcast(U16).rearrange("g o (t p) -> g o t p", t=PACK)[
-                        :, :, :, j * HALF : (j + 1) * HALF
-                    ],
-                    kw_got[u][j][:]
-                    .rearrange("g t p -> g (t p)")
-                    .bitcast(U16)
-                    .rearrange("g (t p o) -> g o t p", t=PACK, o=DP),
-                )
-
-        def key_biases(u, got):
-            nc.vector.tensor_copy(by_column(got), kb_win[:].bitcast(U32).indirect(lists(u)))
-            to_columns(got, kb_col[u])
-
-        def token_scales(u, got):
-            nc.vector.tensor_copy(by_column(got), vs_win[:].bitcast(U32).indirect(lists(u)))
-            to_columns(got, vs_col[u])
+        def keys(u):
+            nc.vector.tensor_copy(
+                kw_got[u][:].rearrange("g t p -> g p t"), kw_win[:, : (REACH, T)[u]].indirect(lists(u))
+            )
+            nc.vector.tensor_copy(
+                k_codes[u][:].bitcast(U16),
+                kw_got[u][:].rearrange("g t p -> g (t p)").bitcast(U16).rearrange("g (s o) -> g o s", o=DP),
+            )
 
         def scores(u, h):
             cols = slice(h * P, (h + 1) * P)
-            bank = score_ps.tile([P, PACK, P], F32, name="bank", tag="score")
+            bank = psum.tile([P, PACK, P], F32, name="bank%d%d" % (u, h))
             for o in range(DP):
                 for t in range(PACK):
                     nc.tensor.matmul_mx(
                         out=bank[:, t, :],
                         lhsT=k_codes[u][:, o, 2 * P * t : 2 * P * (t + 1)].bitcast(FP4X4),
-                        lhsT_scale=k_plane[o][:, PASS * u + P * t : PASS * u + P * (t + 1)],
+                        lhsT_scale=k_plane[:, o, PASS * u + P * t : PASS * u + P * (t + 1)],
                         rhs=q_codes[:, o, cols].bitcast(FP8X4),
                         rhs_scale=q_plane[:, o, cols],
                         start=(o == 0 and t == 0),
                         stop=(o == DP - 1 and t == PACK - 1),
                     )
             for t in range(PACK):
-                nc.scalar.activation(prob[u][:, t, cols], bank[:, t, :], SIGMOID, bias=kb_col[u][:, t : t + 1])
+                nc.scalar.activation(prob[u][h][:, t, :], bank[:, t, :], SIGMOID, bias=kb_col[u][:, t : t + 1])
 
-        def gather_values(u):
-            nc.scalar.activation(
-                v_got[u][:].rearrange("e t (m i) -> e m t i", i=4), v_win[:, : (REACH, T)[u]].indirect(lists(u)), COPY
-            )
-
-        def turn_values(u, turned):
-            for t in range(PACK):
-                nc.tensor.transpose(turned[:, t, :], v_got[u][:, t, :], ident[:])
+        def turn_values(u):
+            turned = psum.tile([P, 2, DV], F32, name="turned%d" % u)
+            words = v_got[u][:].bitcast(F32)
+            for j in range(2):
+                nc.tensor.transpose(turned[:, j, :], words[:, j::2], ident[:])
             nc.scalar.copy(
-                v_bf[:, u].rearrange("p (c i) t -> p c t i", i=4), turned[:].rearrange("p t (c i) -> p c t i", i=4)
+                v_bf[:, u].rearrange("p e t -> p (e t)").bitcast(F32).rearrange("p (e j) -> p e j", j=2),
+                turned[:].rearrange("p j e -> p e j"),
             )
 
         def weights(u, h):
-            cols = slice(h * P, (h + 1) * P)
             nc.vector.tensor_tensor(
-                w_bf[u][:, cols, :].rearrange("p (c i) t -> p c t i", i=4),
-                prob[u][:, :, cols].rearrange("p t (c i) -> p c t i", i=4),
+                w_bf[u][h][:].rearrange("p (c i) t -> p c t i", i=4),
+                prob[u][h][:].rearrange("p t (c i) -> p c t i", i=4),
                 vs_col[u][:].unsqueeze(1).unsqueeze(3).to_broadcast([P, P // 4, PACK, 4]),
                 MULT,
             )
@@ -198,44 +159,38 @@ def tile_attend_sigm_kb_gate_srtq256n1024t2048_kernel(
             nc.vector.quantize_mx(
                 out=w_codes[u][:, cols].bitcast(FP8X4),
                 scales=w_plane[u][:, cols],
-                in_=w_bf[u][:, cols, :].rearrange("p q t -> p (q t)"),
+                in_=w_bf[u][h][:].rearrange("p q t -> p (q t)"),
             )
 
+        row_gather(kb_win, kb_got[0], kb_col[0], 0)
         key_scales()
-        gather_values(0)
-        nc.scalar.copy(v_win[:, REACH:], v_tail[:])
-        gather_values(1)
-        turn_values(0, turn_ps.tile([P, PACK, DV], BF16, name="turned0", tag="turn"))
-        early = keep.tile([P, 2, PASS], F32, name="early")
-        key_biases(0, early[:, 0, :])
-        token_scales(0, early[:, 1, :])
-        key_words(0)
-        part_words(0)
-        late_kb = keep.tile([P, PASS], F32, name="late_kb", tag="got00")
-        key_biases(1, late_kb[:])
-        key_words(1)
-        part_words(1)
-        late_vs = keep.tile([P, PASS], F32, name="late_vs", tag="got10")
-        token_scales(1, late_vs[:])
+        row_gather(kb_win, kb_got[1], kb_col[1], 1)
+        row_gather(vs_win, vs_got[0], vs_col[0], 0)
+        row_gather(vs_win, vs_got[1], vs_col[1], 1)
+        keys(0)
+        keys(1)
         scores(0, 0)
+        nc.vector.tensor_copy(v_got[1][:], v_win[:].indirect(lists(1)))
+        nc.scalar.activation(v_got[0][:], v_win[:].indirect(lists(0)), COPY)
         scores(0, 1)
         scores(1, 0)
-        turn_values(1, score_ps.tile([P, PACK, P], BF16, name="turned1", tag="score"))
         scores(1, 1)
-        acc = [turn_ps.tile([P, DV], F32, name="acc%d" % h, tag="turn") for h in range(QH)]
-        result = [keep.tile([P, DV], F32, name="result%d" % h) for h in range(QH)]
-        v_codes = keep.tile([P, SP, DV], U32, name="v_codes", tag="scales", align_bytes=64)
+        turn_values(0)
+        turn_values(1)
+        acc = [psum.tile([P, DV], F32, name="acc%d" % h) for h in range(QH)]
         for u in range(SP):
-            weights(u, 0)
-            if u == 0:
+            for h in range(QH):
+                weights(u, h)
+            if u == 1:
                 nc.vector.quantize_mx(
                     out=v_codes[:].rearrange("p u e -> p (u e)").bitcast(FP8X4),
                     scales=v_plane[:].rearrange("p u e -> p (u e)"),
                     in_=v_bf[:].rearrange("p u e t -> p (u e t)"),
                 )
-            weights(u, 1)
             for h in range(QH):
                 quantise_w(u, h)
+        for h in range(QH):
+            for u in range(SP):
                 nc.tensor.matmul_mx(
                     out=acc[h][:],
                     lhsT=w_codes[u][:, h * P : (h + 1) * P].bitcast(FP8X4),
@@ -245,6 +200,5 @@ def tile_attend_sigm_kb_gate_srtq256n1024t2048_kernel(
                     start=(u == 0),
                     stop=(u == SP - 1),
                 )
-        for h in range(QH):
             nc.vector.scalar_tensor_tensor(result[h][:], acc[h][:], 1.0 / 16.0, gate[:, h, :], MULT, MULT)
             nc.sync.dma_start(out[0, h * P : (h + 1) * P, :], result[h][:])

@@ -28,6 +28,7 @@ COLS = PASS // 16
 REACH = T - N + PASS
 ROW = P - 1
 KS0 = 96
+HALF = P // 2
 
 
 def tile_attend_sigm_kb_gate_srtq256n1024t2048_kernel(
@@ -36,33 +37,30 @@ def tile_attend_sigm_kb_gate_srtq256n1024t2048_kernel(
     nc = tc.nc
     with ExitStack() as ctx:
         keep = ctx.enter_context(tc.tile_pool(name="keep", bufs=1))
+        reuse = ctx.enter_context(tc.tile_pool(name="reuse", bufs=1))
         psum = ctx.enter_context(tc.psum_pool(name="psum", bufs=1))
 
         offsets = keep.tile([P, N // 16], U16, name="offsets")
         kw_win = keep.tile([P, T], U32, name="kw_win")
         ks_win = keep.tile([P, T], U8, name="ks_win")
         kb_win = keep.tile([P, T], F32, name="kb_win")
-        vs_win = keep.tile([P, T], F32, name="vs_win")
         q_codes = keep.tile([P, DP, NQ], U32, name="q_codes", align_bytes=64)
         q_plane = keep.tile([P, DP, NQ], U8, name="q_plane", align_bytes=64)
         k_plane = keep.tile([P, DP, N], U8, name="k_plane", align_bytes=64)
-        og_raw = keep.tile([P, QH, DV], F32, name="og_raw", tag="og")
+        og_raw = reuse.tile([P, QH, DV], F32, name="og_raw", offset=0)
+        v_win = keep.tile([P, T], F32, name="v_win")
         gate = keep.tile([P, QH, DV], F32, name="gate")
-        ident = keep.tile([P, P], F32, name="ident")
 
-        nc.gpsimd.memset(q_plane[:].bitcast(I32), 0)
-        nc.gpsimd.memset(k_plane[:].bitcast(I32), 0)
-        make_identity(nc, ident[:])
+        nc.vector.memset(q_plane[:].bitcast(I32), 0)
         nc.vector.memset(ks_win[:KS0, :].bitcast(I32), 0)
         nc.vector.memset(kb_win[:ROW, :], 0.0)
-        nc.vector.memset(vs_win[:ROW, :], 0.0)
+        nc.vector.memset(k_plane[:].bitcast(I32), 0)
 
         k_rows = k_words[0].rearrange("p t b -> p (t b)").bitcast(I32)
         nc.sync.dma_start(offsets[:], offs)
         nc.sync.dma_start(ks_win[KS0:, :].bitcast(I32), k_scales.rearrange("o f t -> f o t").bitcast(I32))
         nc.sync.dma_start(og_raw[:], og[0].rearrange("(h p) e -> p h e", p=P))
         nc.sync.dma_start(kb_win[ROW:, :], kb[0:1, :])
-        nc.sync.dma_start(vs_win[ROW:, :], vs[0:1, :])
         nc.sync.dma_start(q_codes[:].bitcast(I32), q_words[0].rearrange("o p q r -> p o (q r)").bitcast(I32))
         nc.sync.dma_start(kw_win[:, :REACH].bitcast(I32), k_rows[:, :REACH])
         for quad in range(4):
@@ -70,17 +68,22 @@ def tile_attend_sigm_kb_gate_srtq256n1024t2048_kernel(
                 q_plane[32 * quad : 32 * quad + 4, :, :].bitcast(I32),
                 q_scales[0][:, 4 * quad : 4 * quad + 4, :].rearrange("o f q -> f o q").bitcast(I32),
             )
-        nc.sync.dma_start(kw_win[:, REACH:].bitcast(I32), k_rows[:, REACH:])
 
         nc.scalar.activation(gate[:], og_raw[:], SIGMOID)
-        v_win = keep.tile([P, T], F32, name="v_win", tag="og")
-        nc.scalar.dma_start(v_win[:], vT)
+        vs_win = reuse.tile([P, T], F32, name="vs_win", offset=512)
+        ident = reuse.tile([P, P], F32, name="ident", offset=0)
+        nc.gpsimd.memset(vs_win[:ROW, :REACH], 0.0)
+        nc.gpsimd.memset(vs_win[:ROW, REACH:], 0.0)
+        make_identity(nc, ident[:])
+        nc.sync.dma_start(vs_win[ROW:, :], vs[0:1, :])
+        nc.sync.dma_start(kw_win[:, REACH:].bitcast(I32), k_rows[:, REACH:])
+        nc.sync.dma_start(v_win[:, : T // 2], vT[:, : T // 2])
 
         def lists(u):
             return offsets[:, u * COLS : (u + 1) * COLS]
 
         ks_got = keep.tile([P, N], U8, name="ks_got")
-        kw_got = [keep.tile([P, PACK, P], U32, name="kw_got%d" % u) for u in range(SP)]
+        kw_got = [[keep.tile([P, PACK, HALF], U32, name="kw_got%d%d" % (u, j)) for j in range(2)] for u in range(SP)]
         k_codes = [keep.tile([P, DP, 2 * PASS], U8, name="k_codes%d" % u, align_bytes=64) for u in range(SP)]
         kb_got = [keep.tile([P, PASS], F32, name="kb_got%d" % u) for u in range(SP)]
         vs_got = [keep.tile([P, PASS], F32, name="vs_got%d" % u) for u in range(SP)]
@@ -97,7 +100,7 @@ def tile_attend_sigm_kb_gate_srtq256n1024t2048_kernel(
         result = [keep.tile([P, DV], F32, name="result%d" % h) for h in range(QH)]
 
         def row_gather(win, got, col, u):
-            nc.scalar.activation(got[:], win[:].indirect(lists(u)), COPY)
+            nc.scalar.activation(got[:], win[:, : (REACH, T)[u]].indirect(lists(u)), COPY)
             nc.sync.dma_start(col[:], got[ROW:, :].rearrange("o (p t) -> o p t", t=PACK))
 
         def key_scales():
@@ -111,13 +114,22 @@ def tile_attend_sigm_kb_gate_srtq256n1024t2048_kernel(
                 )
 
         def keys(u):
-            nc.vector.tensor_copy(
-                kw_got[u][:].rearrange("g t p -> g p t"), kw_win[:, : (REACH, T)[u]].indirect(lists(u))
-            )
-            nc.vector.tensor_copy(
-                k_codes[u][:].bitcast(U16),
-                kw_got[u][:].rearrange("g t p -> g (t p)").bitcast(U16).rearrange("g (s o) -> g o s", o=DP),
-            )
+            for j in range(2):
+                first = u * COLS + j * COLS // 2
+                nc.vector.tensor_copy(
+                    kw_got[u][j][:].rearrange("g t p -> g p t"),
+                    kw_win[:, : (REACH, T)[u]].indirect(offsets[:, first : first + COLS // 2]),
+                )
+            for j in range(2):
+                nc.vector.tensor_copy(
+                    k_codes[u][:].bitcast(U16).rearrange("g o (t p) -> g o t p", t=PACK)[
+                        :, :, :, j * HALF : (j + 1) * HALF
+                    ],
+                    kw_got[u][j][:]
+                    .rearrange("g t p -> g (t p)")
+                    .bitcast(U16)
+                    .rearrange("g (t p o) -> g o t p", t=PACK, o=DP),
+                )
 
         def scores(u, h):
             cols = slice(h * P, (h + 1) * P)
@@ -165,14 +177,15 @@ def tile_attend_sigm_kb_gate_srtq256n1024t2048_kernel(
         row_gather(kb_win, kb_got[0], kb_col[0], 0)
         key_scales()
         row_gather(kb_win, kb_got[1], kb_col[1], 1)
+        nc.sync.dma_start(v_win[:, T // 2 :], vT[:, T // 2 :])
         row_gather(vs_win, vs_got[0], vs_col[0], 0)
         row_gather(vs_win, vs_got[1], vs_col[1], 1)
         keys(0)
         keys(1)
         scores(0, 0)
         nc.vector.tensor_copy(v_got[1][:], v_win[:].indirect(lists(1)))
-        nc.scalar.activation(v_got[0][:], v_win[:].indirect(lists(0)), COPY)
         scores(0, 1)
+        nc.scalar.activation(v_got[0][:], v_win[:].indirect(lists(0)), COPY)
         scores(1, 0)
         scores(1, 1)
         turn_values(0)

@@ -37,7 +37,6 @@ def tile_attend_sigm_kb_gate_srtq256n1024t2048_kernel(
     nc = tc.nc
     with ExitStack() as ctx:
         keep = ctx.enter_context(tc.tile_pool(name="keep", bufs=1))
-        reuse = ctx.enter_context(tc.tile_pool(name="reuse", bufs=1))
         psum = ctx.enter_context(tc.psum_pool(name="psum", bufs=1))
 
         offsets = keep.tile([P, N // 16], U16, name="offsets")
@@ -47,43 +46,46 @@ def tile_attend_sigm_kb_gate_srtq256n1024t2048_kernel(
         q_codes = keep.tile([P, DP, NQ], U32, name="q_codes", align_bytes=64)
         q_plane = keep.tile([P, DP, NQ], U8, name="q_plane", align_bytes=64)
         k_plane = keep.tile([P, DP, N], U8, name="k_plane", align_bytes=64)
-        og_raw = reuse.tile([P, QH, DV], F32, name="og_raw", offset=0)
+        og_raw = keep.tile([P, QH, DV], F32, name="og_raw")
+        vs_win = keep.tile([P, T], F32, name="vs_win")
+        ident = keep.tile([P, P], F32, name="ident")
         v_win = keep.tile([P, T], F32, name="v_win")
         gate = keep.tile([P, QH, DV], F32, name="gate")
 
-        nc.vector.memset(q_plane[:].bitcast(I32), 0)
-        nc.vector.memset(ks_win[:KS0, :].bitcast(I32), 0)
-        nc.vector.memset(kb_win[:ROW, :], 0.0)
-        nc.vector.memset(k_plane[:].bitcast(I32), 0)
+        def zero_odd(words):
+            cut = words.shape[1] // 2 - 1
+            nc.vector.memset(words[:, :cut], 0)
+            nc.vector.memset(words[:, cut:], 0)
+
+        nc.gpsimd.memset(kb_win[:ROW, :], 0.0)
+        nc.gpsimd.memset(vs_win[:ROW, :], 0.0)
+        make_identity(nc, ident[:])
+        zero_odd(q_plane[:].rearrange("p o q -> p (o q)").bitcast(I32))
+        zero_odd(ks_win[:KS0, :].bitcast(I32))
+        zero_odd(k_plane[:].rearrange("p o n -> p (o n)").bitcast(I32))
 
         k_rows = k_words[0].rearrange("p t b -> p (t b)").bitcast(I32)
         nc.sync.dma_start(offsets[:], offs)
         nc.sync.dma_start(ks_win[KS0:, :].bitcast(I32), k_scales.rearrange("o f t -> f o t").bitcast(I32))
         nc.sync.dma_start(og_raw[:], og[0].rearrange("(h p) e -> p h e", p=P))
         nc.sync.dma_start(kb_win[ROW:, :], kb[0:1, :])
-        nc.sync.dma_start(q_codes[:].bitcast(I32), q_words[0].rearrange("o p q r -> p o (q r)").bitcast(I32))
-        nc.sync.dma_start(kw_win[:, :REACH].bitcast(I32), k_rows[:, :REACH])
+        nc.sync.dma_start(vs_win[ROW:, :], vs[0:1, :])
+        nc.sync.dma_start(kw_win[:].bitcast(I32), k_rows)
         for quad in range(4):
             nc.sync.dma_start(
                 q_plane[32 * quad : 32 * quad + 4, :, :].bitcast(I32),
                 q_scales[0][:, 4 * quad : 4 * quad + 4, :].rearrange("o f q -> f o q").bitcast(I32),
             )
+        nc.sync.dma_start(q_codes[:].bitcast(I32), q_words[0].rearrange("o p q r -> p o (q r)").bitcast(I32))
 
         nc.scalar.activation(gate[:], og_raw[:], SIGMOID)
-        vs_win = reuse.tile([P, T], F32, name="vs_win", offset=512)
-        ident = reuse.tile([P, P], F32, name="ident", offset=0)
-        nc.gpsimd.memset(vs_win[:ROW, :REACH], 0.0)
-        nc.gpsimd.memset(vs_win[:ROW, REACH:], 0.0)
-        make_identity(nc, ident[:])
-        nc.sync.dma_start(vs_win[ROW:, :], vs[0:1, :])
-        nc.sync.dma_start(kw_win[:, REACH:].bitcast(I32), k_rows[:, REACH:])
-        nc.sync.dma_start(v_win[:, : T // 2], vT[:, : T // 2])
+        nc.sync.dma_start(v_win[:, :REACH], vT[:, :REACH])
 
         def lists(u):
             return offsets[:, u * COLS : (u + 1) * COLS]
 
         ks_got = keep.tile([P, N], U8, name="ks_got")
-        kw_got = [[keep.tile([P, PACK, HALF], U32, name="kw_got%d%d" % (u, j)) for j in range(2)] for u in range(SP)]
+        kw_got = [[keep.tile([P, PACK, HALF], U32, name="kw_got%d%d" % (u, j), tag="got%d%d" % (u, j)) for j in range(2)] for u in range(SP)]
         k_codes = [keep.tile([P, DP, 2 * PASS], U8, name="k_codes%d" % u, align_bytes=64) for u in range(SP)]
         kb_got = [keep.tile([P, PASS], F32, name="kb_got%d" % u) for u in range(SP)]
         vs_got = [keep.tile([P, PASS], F32, name="vs_got%d" % u) for u in range(SP)]
@@ -93,7 +95,6 @@ def tile_attend_sigm_kb_gate_srtq256n1024t2048_kernel(
         w_bf = [[keep.tile([P, P, PACK], BF16, name="w_bf%d%d" % (u, h), align_bytes=64) for h in range(QH)] for u in range(SP)]
         w_codes = [keep.tile([P, NQ], U32, name="w_codes%d" % u, align_bytes=64) for u in range(SP)]
         w_plane = [keep.tile([P, NQ], U8, name="w_plane%d" % u, align_bytes=64) for u in range(SP)]
-        v_got = [keep.tile([P, PASS], BF16, name="v_got%d" % u) for u in range(SP)]
         v_bf = keep.tile([P, SP, DV, PACK], BF16, name="v_bf", align_bytes=64)
         v_codes = keep.tile([P, SP, DV], U32, name="v_codes", align_bytes=64)
         v_plane = keep.tile([P, SP, DV], U8, name="v_plane", align_bytes=64)
@@ -118,7 +119,7 @@ def tile_attend_sigm_kb_gate_srtq256n1024t2048_kernel(
                 first = u * COLS + j * COLS // 2
                 nc.vector.tensor_copy(
                     kw_got[u][j][:].rearrange("g t p -> g p t"),
-                    kw_win[:, : (REACH, T)[u]].indirect(offsets[:, first : first + COLS // 2]),
+                    kw_win[:].indirect(offsets[:, first : first + COLS // 2]),
                 )
             for j in range(2):
                 nc.vector.tensor_copy(
@@ -176,32 +177,39 @@ def tile_attend_sigm_kb_gate_srtq256n1024t2048_kernel(
 
         row_gather(kb_win, kb_got[0], kb_col[0], 0)
         key_scales()
+        nc.sync.dma_start(v_win[:, REACH:], vT[:, REACH:])
         row_gather(kb_win, kb_got[1], kb_col[1], 1)
-        nc.sync.dma_start(v_win[:, T // 2 :], vT[:, T // 2 :])
         row_gather(vs_win, vs_got[0], vs_col[0], 0)
         row_gather(vs_win, vs_got[1], vs_col[1], 1)
         keys(0)
         keys(1)
-        scores(0, 0)
+        v_got = [keep.tile([P, PASS], BF16, name="v_got0"), keep.tile([P, PASS], BF16, name="v_got1", tag="got10")]
         nc.vector.tensor_copy(v_got[1][:], v_win[:].indirect(lists(1)))
-        scores(0, 1)
-        nc.scalar.activation(v_got[0][:], v_win[:].indirect(lists(0)), COPY)
+        for h in range(QH):
+            nc.scalar.activation(
+                v_got[0][:, h * PASS // 2 : (h + 1) * PASS // 2],
+                v_win[:].indirect(offsets[:, h * COLS // 2 : (h + 1) * COLS // 2]),
+                COPY,
+            )
+            scores(0, h)
         scores(1, 0)
         scores(1, 1)
         turn_values(0)
         turn_values(1)
         acc = [psum.tile([P, DV], F32, name="acc%d" % h) for h in range(QH)]
-        for u in range(SP):
-            for h in range(QH):
-                weights(u, h)
-            if u == 1:
-                nc.vector.quantize_mx(
-                    out=v_codes[:].rearrange("p u e -> p (u e)").bitcast(FP8X4),
-                    scales=v_plane[:].rearrange("p u e -> p (u e)"),
-                    in_=v_bf[:].rearrange("p u e t -> p (u e t)"),
-                )
-            for h in range(QH):
-                quantise_w(u, h)
+        weights(0, 0)
+        weights(0, 1)
+        quantise_w(0, 0)
+        weights(1, 0)
+        quantise_w(0, 1)
+        quantise_w(1, 0)
+        weights(1, 1)
+        nc.vector.quantize_mx(
+            out=v_codes[:].rearrange("p u e -> p (u e)").bitcast(FP8X4),
+            scales=v_plane[:].rearrange("p u e -> p (u e)"),
+            in_=v_bf[:].rearrange("p u e t -> p (u e t)"),
+        )
+        quantise_w(1, 1)
         for h in range(QH):
             for u in range(SP):
                 nc.tensor.matmul_mx(

@@ -60,6 +60,9 @@ def tile_attend_sigm_kb_gate_srtq256n1024t2048_kernel(
         nc.gpsimd.memset(kb_win[:ROW, :], 0.0)
         nc.gpsimd.memset(vs_win[:ROW, :], 0.0)
         make_identity(nc, ident[:])
+        warm = keep.tile([P, 2], F32, name="warm")
+        nc.vector.memset(warm[:, 0:1], 0.0)
+        nc.scalar.activation(warm[:, 1:2], warm[:, 0:1], SIGMOID)
         zero_odd(q_plane[:].rearrange("p o q -> p (o q)").bitcast(I32))
         zero_odd(ks_win[:KS0, :].bitcast(I32))
         zero_odd(k_plane[:].rearrange("p o n -> p (o n)").bitcast(I32))
@@ -67,31 +70,28 @@ def tile_attend_sigm_kb_gate_srtq256n1024t2048_kernel(
         k_rows = k_words[0].rearrange("p t b -> p (t b)").bitcast(I32)
         nc.sync.dma_start(offsets[:], offs)
         nc.sync.dma_start(ks_win[KS0:, :].bitcast(I32), k_scales.rearrange("o f t -> f o t").bitcast(I32))
-        nc.sync.dma_start(og_raw[:], og[0].rearrange("(h p) e -> p h e", p=P))
         nc.sync.dma_start(kb_win[ROW:, :], kb[0:1, :])
         nc.sync.dma_start(vs_win[ROW:, :], vs[0:1, :])
-        nc.sync.dma_start(kw_win[:].bitcast(I32), k_rows)
+        nc.sync.dma_start(kw_win[:, :REACH].bitcast(I32), k_rows[:, :REACH])
         for quad in range(4):
             nc.sync.dma_start(
                 q_plane[32 * quad : 32 * quad + 4, :, :].bitcast(I32),
                 q_scales[0][:, 4 * quad : 4 * quad + 4, :].rearrange("o f q -> f o q").bitcast(I32),
             )
         nc.sync.dma_start(q_codes[:].bitcast(I32), q_words[0].rearrange("o p q r -> p o (q r)").bitcast(I32))
-
-        nc.scalar.activation(gate[:], og_raw[:], SIGMOID)
-        nc.sync.dma_start(v_win[:, :REACH], vT[:, :REACH])
+        nc.sync.dma_start(kw_win[:, REACH:].bitcast(I32), k_rows[:, REACH:])
+        nc.sync.dma_start(v_win[:, : T // 2], vT[:, : T // 2])
 
         def lists(u):
             return offsets[:, u * COLS : (u + 1) * COLS]
 
         ks_got = keep.tile([P, N], U8, name="ks_got")
-        kw_got = [[keep.tile([P, PACK, HALF], U32, name="kw_got%d%d" % (u, j), tag="got%d%d" % (u, j)) for j in range(2)] for u in range(SP)]
-        k_codes = [keep.tile([P, DP, 2 * PASS], U8, name="k_codes%d" % u, align_bytes=64) for u in range(SP)]
+        k_codes = [keep.tile([P, DP, 2 * PASS], U8, name="k_codes%d" % u, tag="codes%d" % u, align_bytes=64) for u in range(SP)]
         kb_got = [keep.tile([P, PASS], F32, name="kb_got%d" % u) for u in range(SP)]
         vs_got = [keep.tile([P, PASS], F32, name="vs_got%d" % u) for u in range(SP)]
         kb_col = [keep.tile([P, PACK], F32, name="kb_col%d" % u) for u in range(SP)]
         vs_col = [keep.tile([P, PACK], F32, name="vs_col%d" % u) for u in range(SP)]
-        prob = [[keep.tile([P, PACK, P], F32, name="prob%d%d" % (u, h)) for h in range(QH)] for u in range(SP)]
+        prob = [[keep.tile([P, PACK, P], F32, name="prob%d%d" % (u, h), tag="prob%d%d" % (u, h)) for h in range(QH)] for u in range(SP)]
         w_bf = [[keep.tile([P, P, PACK], BF16, name="w_bf%d%d" % (u, h), align_bytes=64) for h in range(QH)] for u in range(SP)]
         w_codes = [keep.tile([P, NQ], U32, name="w_codes%d" % u, align_bytes=64) for u in range(SP)]
         w_plane = [keep.tile([P, NQ], U8, name="w_plane%d" % u, align_bytes=64) for u in range(SP)]
@@ -100,9 +100,11 @@ def tile_attend_sigm_kb_gate_srtq256n1024t2048_kernel(
         v_plane = keep.tile([P, SP, DV], U8, name="v_plane", align_bytes=64)
         result = [keep.tile([P, DV], F32, name="result%d" % h) for h in range(QH)]
 
-        def row_gather(win, got, col, u):
-            nc.scalar.activation(got[:], win[:, : (REACH, T)[u]].indirect(lists(u)), COPY)
-            nc.sync.dma_start(col[:], got[ROW:, :].rearrange("o (p t) -> o p t", t=PACK))
+        def row_gather(win, got, u):
+            nc.scalar.activation(got[u][:], win[:].indirect(lists(u)), COPY)
+
+        def to_columns(got, col, u):
+            nc.sync.dma_start(col[u][:], got[u][ROW:, :].rearrange("o (p t) -> o p t", t=PACK))
 
         def key_scales():
             nc.vector.tensor_copy(
@@ -115,18 +117,19 @@ def tile_attend_sigm_kb_gate_srtq256n1024t2048_kernel(
                 )
 
         def keys(u):
+            kw_got = [keep.tile([P, PACK, HALF], U32, name="kw_got%d%d" % (u, j), tag="got%d" % j) for j in range(2)]
             for j in range(2):
                 first = u * COLS + j * COLS // 2
                 nc.vector.tensor_copy(
-                    kw_got[u][j][:].rearrange("g t p -> g p t"),
-                    kw_win[:].indirect(offsets[:, first : first + COLS // 2]),
+                    kw_got[j][:].rearrange("g t p -> g p t"),
+                    kw_win[:, : (REACH, T)[u]].indirect(offsets[:, first : first + COLS // 2]),
                 )
             for j in range(2):
                 nc.vector.tensor_copy(
                     k_codes[u][:].bitcast(U16).rearrange("g o (t p) -> g o t p", t=PACK)[
                         :, :, :, j * HALF : (j + 1) * HALF
                     ],
-                    kw_got[u][j][:]
+                    kw_got[j][:]
                     .rearrange("g t p -> g (t p)")
                     .bitcast(U16)
                     .rearrange("g (t p o) -> g o t p", t=PACK, o=DP),
@@ -175,30 +178,35 @@ def tile_attend_sigm_kb_gate_srtq256n1024t2048_kernel(
                 in_=w_bf[u][h][:].rearrange("p q t -> p (q t)"),
             )
 
-        row_gather(kb_win, kb_got[0], kb_col[0], 0)
+        for u in range(SP):
+            row_gather(kb_win, kb_got, u)
+        for u in range(SP):
+            row_gather(vs_win, vs_got, u)
         key_scales()
-        nc.sync.dma_start(v_win[:, REACH:], vT[:, REACH:])
-        row_gather(kb_win, kb_got[1], kb_col[1], 1)
-        row_gather(vs_win, vs_got[0], vs_col[0], 0)
-        row_gather(vs_win, vs_got[1], vs_col[1], 1)
+        to_columns(kb_got, kb_col, 0)
+        nc.sync.dma_start(v_win[:, T // 2 :], vT[:, T // 2 :])
+        to_columns(vs_got, vs_col, 0)
+        to_columns(kb_got, kb_col, 1)
+        to_columns(vs_got, vs_col, 1)
+        nc.sync.dma_start(og_raw[:], og[0].rearrange("(h p) e -> p h e", p=P))
         keys(0)
         keys(1)
-        v_got = [keep.tile([P, PASS], BF16, name="v_got0"), keep.tile([P, PASS], BF16, name="v_got1", tag="got10")]
+        scores(0, 0)
+        scores(0, 1)
+        weights(0, 0)
+        v_got = [
+            keep.tile([P, PASS], BF16, name="v_got0", tag="codes0", align_bytes=64),
+            keep.tile([P, PASS], BF16, name="v_got1", tag="prob00"),
+        ]
+        nc.scalar.activation(v_got[0][:], v_win[:].indirect(lists(0)), COPY)
+        weights(0, 1)
         nc.vector.tensor_copy(v_got[1][:], v_win[:].indirect(lists(1)))
-        for h in range(QH):
-            nc.scalar.activation(
-                v_got[0][:, h * PASS // 2 : (h + 1) * PASS // 2],
-                v_win[:].indirect(offsets[:, h * COLS // 2 : (h + 1) * COLS // 2]),
-                COPY,
-            )
-            scores(0, h)
         scores(1, 0)
         scores(1, 1)
         turn_values(0)
         turn_values(1)
+        nc.scalar.activation(gate[:], og_raw[:], SIGMOID)
         acc = [psum.tile([P, DV], F32, name="acc%d" % h) for h in range(QH)]
-        weights(0, 0)
-        weights(0, 1)
         quantise_w(0, 0)
         weights(1, 0)
         quantise_w(0, 1)

@@ -57,9 +57,9 @@ def tile_attend_sigm_kb_gate_srtq256n1024t2048_kernel(
             nc.vector.memset(words[:, :cut], 0)
             nc.vector.memset(words[:, cut:], 0)
 
-        nc.gpsimd.memset(kb_win[:ROW, :], 0.0)
-        nc.gpsimd.memset(vs_win[:ROW, :], 0.0)
         make_identity(nc, ident[:])
+        nc.gpsimd.memset(vs_win[:ROW, :], 0.0)
+        nc.gpsimd.memset(kb_win[:ROW, :], 0.0)
         warm = keep.tile([P, 2], F32, name="warm")
         nc.vector.memset(warm[:, 0:1], 0.0)
         nc.scalar.activation(warm[:, 1:2], warm[:, 0:1], SIGMOID)
@@ -70,8 +70,8 @@ def tile_attend_sigm_kb_gate_srtq256n1024t2048_kernel(
         k_rows = k_words[0].rearrange("p t b -> p (t b)").bitcast(I32)
         nc.sync.dma_start(offsets[:], offs)
         nc.sync.dma_start(ks_win[KS0:, :].bitcast(I32), k_scales.rearrange("o f t -> f o t").bitcast(I32))
-        nc.sync.dma_start(kb_win[ROW:, :], kb[0:1, :])
         nc.sync.dma_start(vs_win[ROW:, :], vs[0:1, :])
+        nc.sync.dma_start(kb_win[ROW:, :], kb[0:1, :])
         nc.sync.dma_start(kw_win[:, :REACH].bitcast(I32), k_rows[:, :REACH])
         for quad in range(4):
             nc.sync.dma_start(
@@ -80,7 +80,7 @@ def tile_attend_sigm_kb_gate_srtq256n1024t2048_kernel(
             )
         nc.sync.dma_start(q_codes[:].bitcast(I32), q_words[0].rearrange("o p q r -> p o (q r)").bitcast(I32))
         nc.sync.dma_start(kw_win[:, REACH:].bitcast(I32), k_rows[:, REACH:])
-        nc.sync.dma_start(v_win[:, : T // 2], vT[:, : T // 2])
+        nc.sync.dma_start(v_win[:, : T // 4], vT[:, : T // 4])
 
         def lists(u):
             return offsets[:, u * COLS : (u + 1) * COLS]
@@ -90,14 +90,14 @@ def tile_attend_sigm_kb_gate_srtq256n1024t2048_kernel(
         kb_got = [keep.tile([P, PASS], F32, name="kb_got%d" % u) for u in range(SP)]
         vs_got = [keep.tile([P, PASS], F32, name="vs_got%d" % u) for u in range(SP)]
         kb_col = [keep.tile([P, PACK], F32, name="kb_col%d" % u) for u in range(SP)]
-        vs_col = [keep.tile([P, PACK], F32, name="vs_col%d" % u) for u in range(SP)]
+        vs_col = [None, keep.tile([P, PACK], F32, name="vs_col1")]
         prob = [[keep.tile([P, PACK, P], F32, name="prob%d%d" % (u, h), tag="prob%d%d" % (u, h)) for h in range(QH)] for u in range(SP)]
         w_bf = [[keep.tile([P, P, PACK], BF16, name="w_bf%d%d" % (u, h), align_bytes=64) for h in range(QH)] for u in range(SP)]
         w_codes = [keep.tile([P, NQ], U32, name="w_codes%d" % u, align_bytes=64) for u in range(SP)]
         w_plane = [keep.tile([P, NQ], U8, name="w_plane%d" % u, align_bytes=64) for u in range(SP)]
-        v_bf = keep.tile([P, SP, DV, PACK], BF16, name="v_bf", align_bytes=64)
-        v_codes = keep.tile([P, SP, DV], U32, name="v_codes", align_bytes=64)
-        v_plane = keep.tile([P, SP, DV], U8, name="v_plane", align_bytes=64)
+        v_bf = [keep.tile([P, DV, PACK], BF16, name="v_bf%d" % u, align_bytes=64) for u in range(SP)]
+        v_codes = [keep.tile([P, DV], U32, name="v_codes%d" % u, align_bytes=64) for u in range(SP)]
+        v_plane = [keep.tile([P, DV], U8, name="v_plane%d" % u, align_bytes=64) for u in range(SP)]
         result = [keep.tile([P, DV], F32, name="result%d" % h) for h in range(QH)]
 
         def row_gather(win, got, u):
@@ -110,7 +110,7 @@ def tile_attend_sigm_kb_gate_srtq256n1024t2048_kernel(
             nc.vector.tensor_copy(
                 ks_got[:].rearrange("g (u t p) -> g u p t", u=SP, t=PACK), ks_win[:].indirect(offsets[:])
             )
-            for quad in range(4):
+            for quad in (0, 2, 1, 3):
                 nc.sync.dma_start(
                     k_plane[32 * quad : 32 * quad + 4, :, :].bitcast(I32),
                     ks_got[KS0 + 8 * quad : KS0 + 8 * quad + 8, :].bitcast(I32),
@@ -153,12 +153,12 @@ def tile_attend_sigm_kb_gate_srtq256n1024t2048_kernel(
                 nc.scalar.activation(prob[u][h][:, t, :], bank[:, t, :], SIGMOID, bias=kb_col[u][:, t : t + 1])
 
         def turn_values(u):
-            turned = psum.tile([P, 2, DV], F32, name="turned%d" % u)
+            turned = psum.tile([P, 2, DV], F32, name="turned%d" % u, tag="turn%d" % u)
             words = v_got[u][:].bitcast(F32)
             for j in range(2):
                 nc.tensor.transpose(turned[:, j, :], words[:, j::2], ident[:])
             nc.scalar.copy(
-                v_bf[:, u].rearrange("p e t -> p (e t)").bitcast(F32).rearrange("p (e j) -> p e j", j=2),
+                v_bf[u][:].rearrange("p e t -> p (e t)").bitcast(F32).rearrange("p (e j) -> p e j", j=2),
                 turned[:].rearrange("p j e -> p e j"),
             )
 
@@ -166,8 +166,13 @@ def tile_attend_sigm_kb_gate_srtq256n1024t2048_kernel(
             nc.vector.tensor_tensor(
                 w_bf[u][h][:].rearrange("p (c i) t -> p c t i", i=4),
                 prob[u][h][:].rearrange("p t (c i) -> p c t i", i=4),
-                vs_col[u][:].unsqueeze(1).unsqueeze(3).to_broadcast([P, P // 4, PACK, 4]),
+                (vs_turned[:, :, ROW], vs_col[1][:])[u].unsqueeze(1).unsqueeze(3).to_broadcast([P, P // 4, PACK, 4]),
                 MULT,
+            )
+
+        def quantise_v(u):
+            nc.vector.quantize_mx(
+                out=v_codes[u][:].bitcast(FP8X4), scales=v_plane[u][:], in_=v_bf[u][:].rearrange("p e t -> p (e t)")
             )
 
         def quantise_w(u, h):
@@ -179,15 +184,18 @@ def tile_attend_sigm_kb_gate_srtq256n1024t2048_kernel(
             )
 
         for u in range(SP):
-            row_gather(kb_win, kb_got, u)
-        for u in range(SP):
             row_gather(vs_win, vs_got, u)
+        for u in range(SP):
+            row_gather(kb_win, kb_got, u)
+        vs_turned = psum.tile([P, PACK, P], F32, name="vs_turned", tag="turn1")
+        for t in range(PACK):
+            nc.tensor.transpose(vs_turned[:, t, :], vs_got[0][:, t::PACK], ident[:])
         key_scales()
+        to_columns(vs_got, vs_col, 1)
+        nc.sync.dma_start(v_win[:, T // 4 : T // 2], vT[:, T // 4 : T // 2])
         to_columns(kb_got, kb_col, 0)
         nc.sync.dma_start(v_win[:, T // 2 :], vT[:, T // 2 :])
-        to_columns(vs_got, vs_col, 0)
         to_columns(kb_got, kb_col, 1)
-        to_columns(vs_got, vs_col, 1)
         nc.sync.dma_start(og_raw[:], og[0].rearrange("(h p) e -> p h e", p=P))
         keys(0)
         keys(1)
@@ -203,8 +211,8 @@ def tile_attend_sigm_kb_gate_srtq256n1024t2048_kernel(
         nc.vector.tensor_copy(v_got[1][:], v_win[:].indirect(lists(1)))
         scores(1, 0)
         scores(1, 1)
-        turn_values(0)
         turn_values(1)
+        turn_values(0)
         nc.scalar.activation(gate[:], og_raw[:], SIGMOID)
         acc = [psum.tile([P, DV], F32, name="acc%d" % h) for h in range(QH)]
         quantise_w(0, 0)
@@ -212,22 +220,20 @@ def tile_attend_sigm_kb_gate_srtq256n1024t2048_kernel(
         quantise_w(0, 1)
         quantise_w(1, 0)
         weights(1, 1)
-        nc.vector.quantize_mx(
-            out=v_codes[:].rearrange("p u e -> p (u e)").bitcast(FP8X4),
-            scales=v_plane[:].rearrange("p u e -> p (u e)"),
-            in_=v_bf[:].rearrange("p u e t -> p (u e t)"),
-        )
+        quantise_v(1)
+        quantise_v(0)
         quantise_w(1, 1)
         for h in range(QH):
-            for u in range(SP):
+            for step in range(SP):
+                u = (step + h + 1) % SP
                 nc.tensor.matmul_mx(
                     out=acc[h][:],
                     lhsT=w_codes[u][:, h * P : (h + 1) * P].bitcast(FP8X4),
                     lhsT_scale=w_plane[u][:, h * P : (h + 1) * P],
-                    rhs=v_codes[:, u, :].bitcast(FP8X4),
-                    rhs_scale=v_plane[:, u, :],
-                    start=(u == 0),
-                    stop=(u == SP - 1),
+                    rhs=v_codes[u][:].bitcast(FP8X4),
+                    rhs_scale=v_plane[u][:],
+                    start=(step == 0),
+                    stop=(step == SP - 1),
                 )
             nc.vector.scalar_tensor_tensor(result[h][:], acc[h][:], 1.0 / 16.0, gate[:, h, :], MULT, MULT)
             nc.sync.dma_start(out[0, h * P : (h + 1) * P, :], result[h][:])

@@ -43,35 +43,36 @@ def tile_attend_sigm_kb_gate_srtq256n1024t2048_kernel(
         kw_win = keep.tile([P, T], U32, name="kw_win")
         ks_win = keep.tile([P, T], U8, name="ks_win")
         kb_win = keep.tile([P, T], F32, name="kb_win")
+        vs_win = keep.tile([P, T], F32, name="vs_win")
+        v_win = keep.tile([P, T], F32, name="v_win")
         q_codes = keep.tile([P, DP, NQ], U32, name="q_codes", align_bytes=64)
         q_plane = keep.tile([P, DP, NQ], U8, name="q_plane", align_bytes=64)
         k_plane = keep.tile([P, DP, N], U8, name="k_plane", align_bytes=64)
         og_raw = keep.tile([P, QH, DV], F32, name="og_raw")
-        vs_win = keep.tile([P, T], F32, name="vs_win")
-        ident = keep.tile([P, P], F32, name="ident")
-        v_win = keep.tile([P, T], F32, name="v_win")
         gate = keep.tile([P, QH, DV], F32, name="gate")
-
-        def zero_odd(words):
-            cut = words.shape[1] // 2 - 1
-            nc.vector.memset(words[:, :cut], 0)
-            nc.vector.memset(words[:, cut:], 0)
-
-        make_identity(nc, ident[:])
-        nc.gpsimd.memset(vs_win[:ROW, :], 0.0)
-        nc.gpsimd.memset(kb_win[:ROW, :], 0.0)
+        ident = keep.tile([P, P], F32, name="ident")
         warm = keep.tile([P, 2], F32, name="warm")
+
+        def zero_odd(words, zero):
+            cut = words.shape[1] // 2 - 1
+            nc.vector.memset(words[:, :cut], zero)
+            nc.vector.memset(words[:, cut:], zero)
+
         nc.vector.memset(warm[:, 0:1], 0.0)
         nc.scalar.activation(warm[:, 1:2], warm[:, 0:1], SIGMOID)
-        zero_odd(q_plane[:].rearrange("p o q -> p (o q)").bitcast(I32))
-        zero_odd(ks_win[:KS0, :].bitcast(I32))
-        zero_odd(k_plane[:].rearrange("p o n -> p (o n)").bitcast(I32))
+        zero_odd(ks_win[:KS0, :].bitcast(I32), 0)
+        zero_odd(kb_win[:ROW, :REACH], 0.0)
+        nc.gpsimd.memset(q_plane[:].rearrange("p o q -> p (o q)").bitcast(I32), 0)
+        nc.gpsimd.memset(kb_win[:ROW, REACH:], 0.0)
+        nc.gpsimd.memset(k_plane[:].rearrange("p o n -> p (o n)").bitcast(I32), 0)
+        nc.gpsimd.memset(vs_win[:ROW, :], 0.0)
+        make_identity(nc, ident[:])
 
         k_rows = k_words[0].rearrange("p t b -> p (t b)").bitcast(I32)
         nc.sync.dma_start(offsets[:], offs)
         nc.sync.dma_start(ks_win[KS0:, :].bitcast(I32), k_scales.rearrange("o f t -> f o t").bitcast(I32))
-        nc.sync.dma_start(vs_win[ROW:, :], vs[0:1, :])
         nc.sync.dma_start(kb_win[ROW:, :], kb[0:1, :])
+        nc.sync.dma_start(vs_win[ROW:, :], vs[0:1, :])
         nc.sync.dma_start(kw_win[:, :REACH].bitcast(I32), k_rows[:, :REACH])
         for quad in range(4):
             nc.sync.dma_start(
@@ -80,7 +81,7 @@ def tile_attend_sigm_kb_gate_srtq256n1024t2048_kernel(
             )
         nc.sync.dma_start(q_codes[:].bitcast(I32), q_words[0].rearrange("o p q r -> p o (q r)").bitcast(I32))
         nc.sync.dma_start(kw_win[:, REACH:].bitcast(I32), k_rows[:, REACH:])
-        nc.sync.dma_start(v_win[:, : T // 4], vT[:, : T // 4])
+        nc.sync.dma_start(v_win[:, :REACH], vT[:, :REACH])
 
         def lists(u):
             return offsets[:, u * COLS : (u + 1) * COLS]
@@ -90,8 +91,9 @@ def tile_attend_sigm_kb_gate_srtq256n1024t2048_kernel(
         kb_got = [keep.tile([P, PASS], F32, name="kb_got%d" % u) for u in range(SP)]
         vs_got = [keep.tile([P, PASS], F32, name="vs_got%d" % u) for u in range(SP)]
         kb_col = [keep.tile([P, PACK], F32, name="kb_col%d" % u) for u in range(SP)]
-        vs_col = [None, keep.tile([P, PACK], F32, name="vs_col1")]
-        prob = [[keep.tile([P, PACK, P], F32, name="prob%d%d" % (u, h), tag="prob%d%d" % (u, h)) for h in range(QH)] for u in range(SP)]
+        vs_col = [keep.tile([P, PACK], F32, name="vs_col%d" % u) for u in range(SP)]
+        v_got = [keep.tile([P, PASS], BF16, name="v_got%d" % u) for u in range(SP)]
+        prob = [[keep.tile([P, PACK, P], F32, name="prob%d%d" % (u, h)) for h in range(QH)] for u in range(SP)]
         w_bf = [[keep.tile([P, P, PACK], BF16, name="w_bf%d%d" % (u, h), align_bytes=64) for h in range(QH)] for u in range(SP)]
         w_codes = [keep.tile([P, NQ], U32, name="w_codes%d" % u, align_bytes=64) for u in range(SP)]
         w_plane = [keep.tile([P, NQ], U8, name="w_plane%d" % u, align_bytes=64) for u in range(SP)]
@@ -101,7 +103,7 @@ def tile_attend_sigm_kb_gate_srtq256n1024t2048_kernel(
         result = [keep.tile([P, DV], F32, name="result%d" % h) for h in range(QH)]
 
         def row_gather(win, got, u):
-            nc.scalar.activation(got[u][:], win[:].indirect(lists(u)), COPY)
+            nc.scalar.activation(got[u][:], win[:, : (REACH, T)[u]].indirect(lists(u)), COPY)
 
         def to_columns(got, col, u):
             nc.sync.dma_start(col[u][:], got[u][ROW:, :].rearrange("o (p t) -> o p t", t=PACK))
@@ -110,6 +112,8 @@ def tile_attend_sigm_kb_gate_srtq256n1024t2048_kernel(
             nc.vector.tensor_copy(
                 ks_got[:].rearrange("g (u t p) -> g u p t", u=SP, t=PACK), ks_win[:].indirect(offsets[:])
             )
+
+        def scale_moves():
             for quad in (0, 2, 1, 3):
                 nc.sync.dma_start(
                     k_plane[32 * quad : 32 * quad + 4, :, :].bitcast(I32),
@@ -149,14 +153,20 @@ def tile_attend_sigm_kb_gate_srtq256n1024t2048_kernel(
                         start=(o == 0 and t == 0),
                         stop=(o == DP - 1 and t == PACK - 1),
                     )
+            return bank
+
+        def sigmoids(u, h, bank):
             for t in range(PACK):
                 nc.scalar.activation(prob[u][h][:, t, :], bank[:, t, :], SIGMOID, bias=kb_col[u][:, t : t + 1])
 
         def turn_values(u):
-            turned = psum.tile([P, 2, DV], F32, name="turned%d" % u, tag="turn%d" % u)
+            turned = psum.tile([P, 2, DV], F32, name="turned%d" % u)
             words = v_got[u][:].bitcast(F32)
             for j in range(2):
                 nc.tensor.transpose(turned[:, j, :], words[:, j::2], ident[:])
+            return turned
+
+        def copy_values(u, turned):
             nc.scalar.copy(
                 v_bf[u][:].rearrange("p e t -> p (e t)").bitcast(F32).rearrange("p (e j) -> p e j", j=2),
                 turned[:].rearrange("p j e -> p e j"),
@@ -166,7 +176,7 @@ def tile_attend_sigm_kb_gate_srtq256n1024t2048_kernel(
             nc.vector.tensor_tensor(
                 w_bf[u][h][:].rearrange("p (c i) t -> p c t i", i=4),
                 prob[u][h][:].rearrange("p t (c i) -> p c t i", i=4),
-                (vs_turned[:, :, ROW], vs_col[1][:])[u].unsqueeze(1).unsqueeze(3).to_broadcast([P, P // 4, PACK, 4]),
+                vs_col[u][:].unsqueeze(1).unsqueeze(3).to_broadcast([P, P // 4, PACK, 4]),
                 MULT,
             )
 
@@ -183,51 +193,11 @@ def tile_attend_sigm_kb_gate_srtq256n1024t2048_kernel(
                 in_=w_bf[u][h][:].rearrange("p q t -> p (q t)"),
             )
 
-        for u in range(SP):
-            row_gather(vs_win, vs_got, u)
-        for u in range(SP):
-            row_gather(kb_win, kb_got, u)
-        vs_turned = psum.tile([P, PACK, P], F32, name="vs_turned", tag="turn1")
-        for t in range(PACK):
-            nc.tensor.transpose(vs_turned[:, t, :], vs_got[0][:, t::PACK], ident[:])
-        key_scales()
-        to_columns(vs_got, vs_col, 1)
-        nc.sync.dma_start(v_win[:, T // 4 : T // 2], vT[:, T // 4 : T // 2])
-        to_columns(kb_got, kb_col, 0)
-        nc.sync.dma_start(v_win[:, T // 2 :], vT[:, T // 2 :])
-        to_columns(kb_got, kb_col, 1)
-        nc.sync.dma_start(og_raw[:], og[0].rearrange("(h p) e -> p h e", p=P))
-        keys(0)
-        keys(1)
-        scores(0, 0)
-        scores(0, 1)
-        weights(0, 0)
-        v_got = [
-            keep.tile([P, PASS], BF16, name="v_got0", tag="codes0", align_bytes=64),
-            keep.tile([P, PASS], BF16, name="v_got1", tag="prob00"),
-        ]
-        nc.scalar.activation(v_got[0][:], v_win[:].indirect(lists(0)), COPY)
-        weights(0, 1)
-        nc.vector.tensor_copy(v_got[1][:], v_win[:].indirect(lists(1)))
-        scores(1, 0)
-        scores(1, 1)
-        turn_values(1)
-        turn_values(0)
-        nc.scalar.activation(gate[:], og_raw[:], SIGMOID)
-        acc = [psum.tile([P, DV], F32, name="acc%d" % h) for h in range(QH)]
-        quantise_w(0, 0)
-        weights(1, 0)
-        quantise_w(0, 1)
-        quantise_w(1, 0)
-        weights(1, 1)
-        quantise_v(1)
-        quantise_v(0)
-        quantise_w(1, 1)
-        for h in range(QH):
-            for step in range(SP):
-                u = (step + h + 1) % SP
+        def finish(h, order):
+            acc = psum.tile([P, DV], F32, name="acc%d" % h)
+            for step, u in enumerate(order):
                 nc.tensor.matmul_mx(
-                    out=acc[h][:],
+                    out=acc[:],
                     lhsT=w_codes[u][:, h * P : (h + 1) * P].bitcast(FP8X4),
                     lhsT_scale=w_plane[u][:, h * P : (h + 1) * P],
                     rhs=v_codes[u][:].bitcast(FP8X4),
@@ -235,5 +205,42 @@ def tile_attend_sigm_kb_gate_srtq256n1024t2048_kernel(
                     start=(step == 0),
                     stop=(step == SP - 1),
                 )
-            nc.vector.scalar_tensor_tensor(result[h][:], acc[h][:], 1.0 / 16.0, gate[:, h, :], MULT, MULT)
+            nc.vector.scalar_tensor_tensor(result[h][:], acc[:], 1.0 / 16.0, gate[:, h, :], MULT, MULT)
             nc.sync.dma_start(out[0, h * P : (h + 1) * P, :], result[h][:])
+
+        row_gather(kb_win, kb_got, 0)
+        to_columns(kb_got, kb_col, 0)
+        key_scales()
+        scale_moves()
+        nc.sync.dma_start(v_win[:, REACH:], vT[:, REACH:])
+        row_gather(kb_win, kb_got, 1)
+        row_gather(vs_win, vs_got, 0)
+        row_gather(vs_win, vs_got, 1)
+        to_columns(vs_got, vs_col, 0)
+        to_columns(kb_got, kb_col, 1)
+        to_columns(vs_got, vs_col, 1)
+        nc.sync.dma_start(og_raw[:], og[0].rearrange("(h p) e -> p h e", p=P))
+        keys(0)
+        keys(1)
+        nc.scalar.activation(v_got[0][:], v_win[:].indirect(lists(0)), COPY)
+        nc.vector.tensor_copy(v_got[1][:], v_win[:].indirect(lists(1)))
+        sigmoids(0, 0, scores(0, 0))
+        nc.scalar.activation(gate[:], og_raw[:], SIGMOID)
+        sigmoids(0, 1, scores(0, 1))
+        weights(0, 0)
+        weights(0, 1)
+        quantise_w(0, 0)
+        sigmoids(1, 0, scores(1, 0))
+        quantise_w(0, 1)
+        weights(1, 0)
+        sigmoids(1, 1, scores(1, 1))
+        turned = [turn_values(u) for u in range(SP)]
+        for u in range(SP):
+            copy_values(u, turned[u])
+        quantise_w(1, 0)
+        weights(1, 1)
+        quantise_v(0)
+        quantise_v(1)
+        quantise_w(1, 1)
+        finish(0, (0, 1))
+        finish(1, (0, 1))

@@ -29,6 +29,7 @@ REACH = T - N + PASS
 ROW = P - 1
 KS0 = 96
 HALF = P // 2
+KB_CUT = 1152
 
 
 def tile_attend_sigm_kb_gate_srtq256n1024t2048_kernel(
@@ -37,15 +38,16 @@ def tile_attend_sigm_kb_gate_srtq256n1024t2048_kernel(
     nc = tc.nc
     with ExitStack() as ctx:
         keep = ctx.enter_context(tc.tile_pool(name="keep", bufs=1))
+        shared = ctx.enter_context(tc.tile_pool(name="shared", bufs=1))
         psum = ctx.enter_context(tc.psum_pool(name="psum", bufs=1))
 
         offsets = keep.tile([P, N // 16], U16, name="offsets")
-        kw_win = keep.tile([P, T], U32, name="kw_win")
+        kw_win = keep.tile([P, T], U32, name="kw_win", align_bytes=256)
         ks_win = keep.tile([P, T], U8, name="ks_win")
         kb_win = keep.tile([P, T], F32, name="kb_win")
         vs_win = keep.tile([P, T], F32, name="vs_win")
-        v_win = keep.tile([P, T], F32, name="v_win")
-        q_codes = keep.tile([P, DP, NQ], U32, name="q_codes", align_bytes=64)
+        v_win = shared.tile([P, T], F32, name="v_win", align_bytes=256, offset=0)
+        q_codes = keep.tile([P, DP, NQ], U32, name="q_codes", align_bytes=256)
         q_plane = keep.tile([P, DP, NQ], U8, name="q_plane", align_bytes=64)
         k_plane = keep.tile([P, DP, N], U8, name="k_plane", align_bytes=64)
         og_raw = keep.tile([P, QH, DV], F32, name="og_raw")
@@ -61,17 +63,19 @@ def tile_attend_sigm_kb_gate_srtq256n1024t2048_kernel(
         nc.vector.memset(warm[:, 0:1], 0.0)
         nc.scalar.activation(warm[:, 1:2], warm[:, 0:1], SIGMOID)
         zero_odd(ks_win[:KS0, :].bitcast(I32), 0)
-        zero_odd(kb_win[:ROW, :REACH], 0.0)
+        zero_odd(kb_win[:ROW, :KB_CUT], 0.0)
         nc.gpsimd.memset(q_plane[:].rearrange("p o q -> p (o q)").bitcast(I32), 0)
-        nc.gpsimd.memset(kb_win[:ROW, REACH:], 0.0)
+        nc.gpsimd.memset(kb_win[:ROW, KB_CUT:REACH], 0.0)
+        nc.gpsimd.memset(vs_win[:ROW, :REACH], 0.0)
         nc.gpsimd.memset(k_plane[:].rearrange("p o n -> p (o n)").bitcast(I32), 0)
-        nc.gpsimd.memset(vs_win[:ROW, :], 0.0)
         make_identity(nc, ident[:])
+        nc.gpsimd.memset(vs_win[:ROW, REACH:], 0.0)
+        nc.gpsimd.memset(kb_win[:ROW, REACH:], 0.0)
 
         k_rows = k_words[0].rearrange("p t b -> p (t b)").bitcast(I32)
         nc.sync.dma_start(offsets[:], offs)
         nc.sync.dma_start(ks_win[KS0:, :].bitcast(I32), k_scales.rearrange("o f t -> f o t").bitcast(I32))
-        nc.sync.dma_start(kb_win[ROW:, :], kb[0:1, :])
+        nc.sync.dma_start(kb_win[ROW:, :REACH], kb[0:1, :REACH])
         nc.sync.dma_start(vs_win[ROW:, :], vs[0:1, :])
         nc.sync.dma_start(kw_win[:, :REACH].bitcast(I32), k_rows[:, :REACH])
         for quad in range(4):
@@ -81,7 +85,7 @@ def tile_attend_sigm_kb_gate_srtq256n1024t2048_kernel(
             )
         nc.sync.dma_start(q_codes[:].bitcast(I32), q_words[0].rearrange("o p q r -> p o (q r)").bitcast(I32))
         nc.sync.dma_start(kw_win[:, REACH:].bitcast(I32), k_rows[:, REACH:])
-        nc.sync.dma_start(v_win[:, :REACH], vT[:, :REACH])
+        nc.sync.dma_start(kb_win[ROW:, REACH:], kb[0:1, REACH:])
 
         def lists(u):
             return offsets[:, u * COLS : (u + 1) * COLS]
@@ -91,11 +95,17 @@ def tile_attend_sigm_kb_gate_srtq256n1024t2048_kernel(
         kb_got = [keep.tile([P, PASS], F32, name="kb_got%d" % u) for u in range(SP)]
         vs_got = [keep.tile([P, PASS], F32, name="vs_got%d" % u) for u in range(SP)]
         kb_col = [keep.tile([P, PACK], F32, name="kb_col%d" % u) for u in range(SP)]
-        vs_col = [keep.tile([P, PACK], F32, name="vs_col%d" % u) for u in range(SP)]
+        vs_col = [None, keep.tile([P, PACK], F32, name="vs_col1")]
         v_got = [keep.tile([P, PASS], BF16, name="v_got%d" % u) for u in range(SP)]
-        prob = [[keep.tile([P, PACK, P], F32, name="prob%d%d" % (u, h)) for h in range(QH)] for u in range(SP)]
+        prob = [
+            [keep.tile([P, PACK, P], F32, name="prob00"), keep.tile([P, PACK, P], F32, name="prob01")],
+            [keep.tile([P, PACK, P], F32, name="prob10"), keep.tile([P, PACK, P], F32, name="prob11")],
+        ]
         w_bf = [[keep.tile([P, P, PACK], BF16, name="w_bf%d%d" % (u, h), align_bytes=64) for h in range(QH)] for u in range(SP)]
-        w_codes = [keep.tile([P, NQ], U32, name="w_codes%d" % u, align_bytes=64) for u in range(SP)]
+        w_codes = [
+            shared.tile([P, NQ], U32, name="w_codes0", offset=4 * PASS),
+            keep.tile([P, NQ], U32, name="w_codes1", align_bytes=64),
+        ]
         w_plane = [keep.tile([P, NQ], U8, name="w_plane%d" % u, align_bytes=64) for u in range(SP)]
         v_bf = [keep.tile([P, DV, PACK], BF16, name="v_bf%d" % u, align_bytes=64) for u in range(SP)]
         v_codes = [keep.tile([P, DV], U32, name="v_codes%d" % u, align_bytes=64) for u in range(SP)]
@@ -160,7 +170,7 @@ def tile_attend_sigm_kb_gate_srtq256n1024t2048_kernel(
                 nc.scalar.activation(prob[u][h][:, t, :], bank[:, t, :], SIGMOID, bias=kb_col[u][:, t : t + 1])
 
         def turn_values(u):
-            turned = psum.tile([P, 2, DV], F32, name="turned%d" % u)
+            turned = psum.tile([P, 2, DV], F32, name="turned%d" % u, tag="turn%d" % u)
             words = v_got[u][:].bitcast(F32)
             for j in range(2):
                 nc.tensor.transpose(turned[:, j, :], words[:, j::2], ident[:])
@@ -176,7 +186,7 @@ def tile_attend_sigm_kb_gate_srtq256n1024t2048_kernel(
             nc.vector.tensor_tensor(
                 w_bf[u][h][:].rearrange("p (c i) t -> p c t i", i=4),
                 prob[u][h][:].rearrange("p t (c i) -> p c t i", i=4),
-                vs_col[u][:].unsqueeze(1).unsqueeze(3).to_broadcast([P, P // 4, PACK, 4]),
+                (vs_turned[:, :, ROW], vs_col[1][:])[u].unsqueeze(1).unsqueeze(3).to_broadcast([P, P // 4, PACK, 4]),
                 MULT,
             )
 
@@ -209,34 +219,37 @@ def tile_attend_sigm_kb_gate_srtq256n1024t2048_kernel(
             nc.sync.dma_start(out[0, h * P : (h + 1) * P, :], result[h][:])
 
         row_gather(kb_win, kb_got, 0)
-        to_columns(kb_got, kb_col, 0)
+        row_gather(vs_win, vs_got, 0)
+        vs_turned = psum.tile([P, PACK, P], F32, name="vs_turned", tag="turn1")
+        for t in range(PACK):
+            nc.tensor.transpose(vs_turned[:, t, :], vs_got[0][:, t::PACK], ident[:])
         key_scales()
         scale_moves()
-        nc.sync.dma_start(v_win[:, REACH:], vT[:, REACH:])
-        row_gather(kb_win, kb_got, 1)
-        row_gather(vs_win, vs_got, 0)
+        to_columns(kb_got, kb_col, 0)
+        nc.sync.dma_start(v_win[:, :REACH], vT[:, :REACH])
         row_gather(vs_win, vs_got, 1)
-        to_columns(vs_got, vs_col, 0)
+        row_gather(kb_win, kb_got, 1)
         to_columns(kb_got, kb_col, 1)
+        nc.sync.dma_start(v_win[:, REACH:], vT[:, REACH:])
         to_columns(vs_got, vs_col, 1)
         nc.sync.dma_start(og_raw[:], og[0].rearrange("(h p) e -> p h e", p=P))
         keys(0)
         keys(1)
-        nc.scalar.activation(v_got[0][:], v_win[:].indirect(lists(0)), COPY)
-        nc.vector.tensor_copy(v_got[1][:], v_win[:].indirect(lists(1)))
         sigmoids(0, 0, scores(0, 0))
-        nc.scalar.activation(gate[:], og_raw[:], SIGMOID)
         sigmoids(0, 1, scores(0, 1))
         weights(0, 0)
         weights(0, 1)
-        quantise_w(0, 0)
         sigmoids(1, 0, scores(1, 0))
-        quantise_w(0, 1)
+        nc.vector.tensor_copy(v_got[0][:], v_win[:].indirect(lists(0)))
+        nc.scalar.activation(v_got[1][:], v_win[:].indirect(lists(1)), COPY)
         weights(1, 0)
+        quantise_w(0, 0)
+        quantise_w(0, 1)
         sigmoids(1, 1, scores(1, 1))
         turned = [turn_values(u) for u in range(SP)]
         for u in range(SP):
             copy_values(u, turned[u])
+        nc.scalar.activation(gate[:], og_raw[:], SIGMOID)
         quantise_w(1, 0)
         weights(1, 1)
         quantise_v(0)

@@ -29,7 +29,7 @@ REACH = T - N + PASS
 ROW = P - 1
 KS0 = 96
 HALF = P // 2
-KB_CUT = 1152
+VS_CUT = 1152
 
 
 def tile_attend_sigm_kb_gate_srtq256n1024t2048_kernel(
@@ -63,29 +63,29 @@ def tile_attend_sigm_kb_gate_srtq256n1024t2048_kernel(
         nc.vector.memset(warm[:, 0:1], 0.0)
         nc.scalar.activation(warm[:, 1:2], warm[:, 0:1], SIGMOID)
         zero_odd(ks_win[:KS0, :].bitcast(I32), 0)
-        zero_odd(kb_win[:ROW, :KB_CUT], 0.0)
+        zero_odd(vs_win[:ROW, :VS_CUT], 0.0)
         nc.gpsimd.memset(q_plane[:].rearrange("p o q -> p (o q)").bitcast(I32), 0)
-        nc.gpsimd.memset(kb_win[:ROW, KB_CUT:REACH], 0.0)
-        nc.gpsimd.memset(vs_win[:ROW, :REACH], 0.0)
-        nc.gpsimd.memset(k_plane[:].rearrange("p o n -> p (o n)").bitcast(I32), 0)
+        nc.gpsimd.memset(vs_win[:ROW, VS_CUT:REACH], 0.0)
+        nc.gpsimd.memset(kb_win[:ROW, :REACH], 0.0)
         make_identity(nc, ident[:])
-        nc.gpsimd.memset(vs_win[:ROW, REACH:], 0.0)
+        nc.gpsimd.memset(k_plane[:].rearrange("p o n -> p (o n)").bitcast(I32), 0)
         nc.gpsimd.memset(kb_win[:ROW, REACH:], 0.0)
+        nc.gpsimd.memset(vs_win[:ROW, REACH:], 0.0)
 
         k_rows = k_words[0].rearrange("p t b -> p (t b)").bitcast(I32)
-        nc.sync.dma_start(offsets[:], offs)
         nc.sync.dma_start(ks_win[KS0:, :].bitcast(I32), k_scales.rearrange("o f t -> f o t").bitcast(I32))
-        nc.sync.dma_start(kb_win[ROW:, :REACH], kb[0:1, :REACH])
-        nc.sync.dma_start(vs_win[ROW:, :], vs[0:1, :])
+        nc.sync.dma_start(offsets[:], offs)
+        nc.sync.dma_start(vs_win[ROW:, :REACH], vs[0:1, :REACH])
+        nc.sync.dma_start(kb_win[ROW:, :], kb[0:1, :])
         nc.sync.dma_start(kw_win[:, :REACH].bitcast(I32), k_rows[:, :REACH])
         for quad in range(4):
             nc.sync.dma_start(
                 q_plane[32 * quad : 32 * quad + 4, :, :].bitcast(I32),
                 q_scales[0][:, 4 * quad : 4 * quad + 4, :].rearrange("o f q -> f o q").bitcast(I32),
             )
+        nc.sync.dma_start(vs_win[ROW:, REACH:], vs[0:1, REACH:])
         nc.sync.dma_start(q_codes[:].bitcast(I32), q_words[0].rearrange("o p q r -> p o (q r)").bitcast(I32))
         nc.sync.dma_start(kw_win[:, REACH:].bitcast(I32), k_rows[:, REACH:])
-        nc.sync.dma_start(kb_win[ROW:, REACH:], kb[0:1, REACH:])
 
         def lists(u):
             return offsets[:, u * COLS : (u + 1) * COLS]
@@ -149,25 +149,22 @@ def tile_attend_sigm_kb_gate_srtq256n1024t2048_kernel(
                     .rearrange("g (t p o) -> g o t p", t=PACK, o=DP),
                 )
 
-        def scores(u, h):
+        def scores(u, h, places, tag):
             cols = slice(h * P, (h + 1) * P)
-            bank = psum.tile([P, PACK, P], F32, name="bank%d%d" % (u, h))
+            bank = psum.tile([P, len(places), P], F32, name="bank%d%d%d" % (u, h, places[0]), tag=tag)
             for o in range(DP):
-                for t in range(PACK):
+                for j, t in enumerate(places):
                     nc.tensor.matmul_mx(
-                        out=bank[:, t, :],
+                        out=bank[:, j, :],
                         lhsT=k_codes[u][:, o, 2 * P * t : 2 * P * (t + 1)].bitcast(FP4X4),
                         lhsT_scale=k_plane[:, o, PASS * u + P * t : PASS * u + P * (t + 1)],
                         rhs=q_codes[:, o, cols].bitcast(FP8X4),
                         rhs_scale=q_plane[:, o, cols],
-                        start=(o == 0 and t == 0),
-                        stop=(o == DP - 1 and t == PACK - 1),
+                        start=(o == 0 and j == 0),
+                        stop=(o == DP - 1 and j == len(places) - 1),
                     )
-            return bank
-
-        def sigmoids(u, h, bank):
-            for t in range(PACK):
-                nc.scalar.activation(prob[u][h][:, t, :], bank[:, t, :], SIGMOID, bias=kb_col[u][:, t : t + 1])
+            for j, t in enumerate(places):
+                nc.scalar.activation(prob[u][h][:, t, :], bank[:, j, :], SIGMOID, bias=kb_col[u][:, t : t + 1])
 
         def turn_values(u):
             turned = psum.tile([P, 2, DV], F32, name="turned%d" % u, tag="turn%d" % u)
@@ -204,7 +201,7 @@ def tile_attend_sigm_kb_gate_srtq256n1024t2048_kernel(
             )
 
         def finish(h, order):
-            acc = psum.tile([P, DV], F32, name="acc%d" % h)
+            acc = psum.tile([P, DV], F32, name="acc%d" % h, tag="acc%d" % h)
             for step, u in enumerate(order):
                 nc.tensor.matmul_mx(
                     out=acc[:],
@@ -218,8 +215,8 @@ def tile_attend_sigm_kb_gate_srtq256n1024t2048_kernel(
             nc.vector.scalar_tensor_tensor(result[h][:], acc[:], 1.0 / 16.0, gate[:, h, :], MULT, MULT)
             nc.sync.dma_start(out[0, h * P : (h + 1) * P, :], result[h][:])
 
-        row_gather(kb_win, kb_got, 0)
         row_gather(vs_win, vs_got, 0)
+        row_gather(kb_win, kb_got, 0)
         vs_turned = psum.tile([P, PACK, P], F32, name="vs_turned", tag="turn1")
         for t in range(PACK):
             nc.tensor.transpose(vs_turned[:, t, :], vs_got[0][:, t::PACK], ident[:])
@@ -227,25 +224,26 @@ def tile_attend_sigm_kb_gate_srtq256n1024t2048_kernel(
         scale_moves()
         to_columns(kb_got, kb_col, 0)
         nc.sync.dma_start(v_win[:, :REACH], vT[:, :REACH])
-        row_gather(vs_win, vs_got, 1)
         row_gather(kb_win, kb_got, 1)
+        row_gather(vs_win, vs_got, 1)
         to_columns(kb_got, kb_col, 1)
         nc.sync.dma_start(v_win[:, REACH:], vT[:, REACH:])
         to_columns(vs_got, vs_col, 1)
         nc.sync.dma_start(og_raw[:], og[0].rearrange("(h p) e -> p h e", p=P))
         keys(0)
         keys(1)
-        sigmoids(0, 0, scores(0, 0))
-        sigmoids(0, 1, scores(0, 1))
+        scores(0, 0, (0, 1), "acc0")
+        scores(0, 0, (2, 3), "acc1")
+        scores(0, 1, range(PACK), "bank01")
         weights(0, 0)
         weights(0, 1)
-        sigmoids(1, 0, scores(1, 0))
+        scores(1, 0, range(PACK), "bank10")
         nc.vector.tensor_copy(v_got[0][:], v_win[:].indirect(lists(0)))
         nc.scalar.activation(v_got[1][:], v_win[:].indirect(lists(1)), COPY)
         weights(1, 0)
         quantise_w(0, 0)
         quantise_w(0, 1)
-        sigmoids(1, 1, scores(1, 1))
+        scores(1, 1, range(PACK), "bank11")
         turned = [turn_values(u) for u in range(SP)]
         for u in range(SP):
             copy_values(u, turned[u])

@@ -30,6 +30,8 @@ ROW = P - 1
 KS0 = 96
 HALF = P // 2
 VS_CUT = 1152
+AHEAD = 320
+SHARE = 64
 
 
 def tile_attend_sigm_kb_gate_srtq256n1024t2048_kernel(
@@ -75,7 +77,7 @@ def tile_attend_sigm_kb_gate_srtq256n1024t2048_kernel(
         k_rows = k_words[0].rearrange("p t b -> p (t b)").bitcast(I32)
         nc.sync.dma_start(ks_win[KS0:, :].bitcast(I32), k_scales.rearrange("o f t -> f o t").bitcast(I32))
         nc.sync.dma_start(offsets[:], offs)
-        nc.sync.dma_start(vs_win[ROW:, :REACH], vs[0:1, :REACH])
+        nc.sync.dma_start(vs_win[ROW:, :], vs[0:1, :])
         nc.sync.dma_start(kb_win[ROW:, :], kb[0:1, :])
         nc.sync.dma_start(kw_win[:, :REACH].bitcast(I32), k_rows[:, :REACH])
         for quad in range(4):
@@ -83,9 +85,9 @@ def tile_attend_sigm_kb_gate_srtq256n1024t2048_kernel(
                 q_plane[32 * quad : 32 * quad + 4, :, :].bitcast(I32),
                 q_scales[0][:, 4 * quad : 4 * quad + 4, :].rearrange("o f q -> f o q").bitcast(I32),
             )
-        nc.sync.dma_start(vs_win[ROW:, REACH:], vs[0:1, REACH:])
         nc.sync.dma_start(q_codes[:].bitcast(I32), q_words[0].rearrange("o p q r -> p o (q r)").bitcast(I32))
         nc.sync.dma_start(kw_win[:, REACH:].bitcast(I32), k_rows[:, REACH:])
+        nc.sync.dma_start(v_win[:, :AHEAD], vT[:, :AHEAD])
 
         def lists(u):
             return offsets[:, u * COLS : (u + 1) * COLS]
@@ -93,7 +95,7 @@ def tile_attend_sigm_kb_gate_srtq256n1024t2048_kernel(
         ks_got = keep.tile([P, N], U8, name="ks_got")
         k_codes = [keep.tile([P, DP, 2 * PASS], U8, name="k_codes%d" % u, tag="codes%d" % u, align_bytes=64) for u in range(SP)]
         kb_got = [keep.tile([P, PASS], F32, name="kb_got%d" % u) for u in range(SP)]
-        vs_got = [keep.tile([P, PASS], F32, name="vs_got%d" % u) for u in range(SP)]
+        vs_got = [keep.tile([P, PASS], F32, name="vs_got0")]
         kb_col = [keep.tile([P, PACK], F32, name="kb_col%d" % u) for u in range(SP)]
         vs_col = [None, keep.tile([P, PACK], F32, name="vs_col1")]
         v_got = [keep.tile([P, PASS], BF16, name="v_got%d" % u) for u in range(SP)]
@@ -131,7 +133,7 @@ def tile_attend_sigm_kb_gate_srtq256n1024t2048_kernel(
                 )
 
         def keys(u):
-            kw_got = [keep.tile([P, PACK, HALF], U32, name="kw_got%d%d" % (u, j), tag="got%d" % j) for j in range(2)]
+            kw_got = [keep.tile([P, PACK, HALF], U32, name="kw_got%d%d" % (u, j), tag="got%d" % (j * (u + 1))) for j in range(2)]
             for j in range(2):
                 first = u * COLS + j * COLS // 2
                 nc.vector.tensor_copy(
@@ -170,7 +172,7 @@ def tile_attend_sigm_kb_gate_srtq256n1024t2048_kernel(
             turned = psum.tile([P, 2, DV], F32, name="turned%d" % u, tag="turn%d" % u)
             words = v_got[u][:].bitcast(F32)
             for j in range(2):
-                nc.tensor.transpose(turned[:, j, :], words[:, j::2], ident[:])
+                nc.tensor.transpose(turned[:, j, :], (words[:, j * P : (j + 1) * P], words[:, j::2])[u], ident[:])
             return turned
 
         def copy_values(u, turned):
@@ -223,23 +225,29 @@ def tile_attend_sigm_kb_gate_srtq256n1024t2048_kernel(
         key_scales()
         scale_moves()
         to_columns(kb_got, kb_col, 0)
-        nc.sync.dma_start(v_win[:, :REACH], vT[:, :REACH])
+        nc.sync.dma_start(v_win[:, AHEAD:REACH], vT[:, AHEAD:REACH])
         row_gather(kb_win, kb_got, 1)
-        row_gather(vs_win, vs_got, 1)
         to_columns(kb_got, kb_col, 1)
         nc.sync.dma_start(v_win[:, REACH:], vT[:, REACH:])
+        keys(0)
+        vs_got.append(keep.tile([P, PASS], F32, name="vs_got1", tag="got1"))
+        row_gather(vs_win, vs_got, 1)
         to_columns(vs_got, vs_col, 1)
         nc.sync.dma_start(og_raw[:], og[0].rearrange("(h p) e -> p h e", p=P))
-        keys(0)
         keys(1)
-        scores(0, 0, (0, 1), "acc0")
-        scores(0, 0, (2, 3), "acc1")
-        scores(0, 1, range(PACK), "bank01")
+        scores(0, 0, (0, 1), "pair0")
+        scores(0, 0, (2, 3), "pair1")
+        scores(0, 1, (0, 1), "acc0")
+        scores(0, 1, (2, 3), "acc1")
         weights(0, 0)
+        nc.vector.tensor_copy(
+            v_got[0][:].rearrange("e (j p t) -> e p j t", j=2, t=2), v_win[:, :REACH].indirect(lists(0))
+        )
         weights(0, 1)
-        scores(1, 0, range(PACK), "bank10")
-        nc.vector.tensor_copy(v_got[0][:], v_win[:].indirect(lists(0)))
-        nc.scalar.activation(v_got[1][:], v_win[:].indirect(lists(1)), COPY)
+        scores(1, 0, (0, 1), "pair0")
+        scores(1, 0, (2, 3), "pair1")
+        nc.vector.tensor_copy(v_got[1][:, :SHARE], v_win[:].indirect(offsets[:, COLS : COLS + SHARE // 16]))
+        nc.scalar.activation(v_got[1][:, SHARE:], v_win[:].indirect(offsets[:, COLS + SHARE // 16 :]), COPY)
         weights(1, 0)
         quantise_w(0, 0)
         quantise_w(0, 1)

@@ -31,7 +31,6 @@ KS0 = 96
 HALF = P // 2
 VS_CUT = 1152
 AHEAD = 320
-SHARE = 64
 
 
 def tile_attend_sigm_kb_gate_srtq256n1024t2048_kernel(
@@ -172,7 +171,7 @@ def tile_attend_sigm_kb_gate_srtq256n1024t2048_kernel(
             turned = psum.tile([P, 2, DV], F32, name="turned%d" % u, tag="turn%d" % u)
             words = v_got[u][:].bitcast(F32)
             for j in range(2):
-                nc.tensor.transpose(turned[:, j, :], (words[:, j * P : (j + 1) * P], words[:, j::2])[u], ident[:])
+                nc.tensor.transpose(turned[:, j, :], words[:, j::2], ident[:])
             return turned
 
         def copy_values(u, turned):
@@ -235,19 +234,17 @@ def tile_attend_sigm_kb_gate_srtq256n1024t2048_kernel(
         to_columns(vs_got, vs_col, 1)
         nc.sync.dma_start(og_raw[:], og[0].rearrange("(h p) e -> p h e", p=P))
         keys(1)
-        scores(0, 0, (0, 1), "pair0")
+        scores(0, 0, (0,), "single")
+        scores(0, 0, (1,), "pair0")
         scores(0, 0, (2, 3), "pair1")
         scores(0, 1, (0, 1), "acc0")
         scores(0, 1, (2, 3), "acc1")
         weights(0, 0)
-        nc.vector.tensor_copy(
-            v_got[0][:].rearrange("e (j p t) -> e p j t", j=2, t=2), v_win[:, :REACH].indirect(lists(0))
-        )
         weights(0, 1)
+        nc.vector.tensor_copy(v_got[0][:], v_win[:].indirect(lists(0)))
         scores(1, 0, (0, 1), "pair0")
         scores(1, 0, (2, 3), "pair1")
-        nc.vector.tensor_copy(v_got[1][:, :SHARE], v_win[:].indirect(offsets[:, COLS : COLS + SHARE // 16]))
-        nc.scalar.activation(v_got[1][:, SHARE:], v_win[:].indirect(offsets[:, COLS + SHARE // 16 :]), COPY)
+        nc.scalar.activation(v_got[1][:], v_win[:].indirect(lists(1)), COPY)
         weights(1, 0)
         quantise_w(0, 0)
         quantise_w(0, 1)

@@ -226,6 +226,9 @@ def tile_attend_sigm_kb_gate_srtq256n1024t2048_kernel(
         to_columns(kb_got, kb_col, 0)
         nc.sync.dma_start(v_win[:, AHEAD:REACH], vT[:, AHEAD:REACH])
         row_gather(kb_win, kb_got, 1)
+        spare = psum.tile([P, PACK, P], F32, name="spare", tag="bank11")
+        for t in range(PACK):
+            nc.tensor.transpose(spare[:, t, :], kb_got[1][:, t * P : (t + 1) * P], ident[:])
         to_columns(kb_got, kb_col, 1)
         nc.sync.dma_start(v_win[:, REACH:], vT[:, REACH:])
         keys(0)

@@ -132,7 +132,7 @@ def tile_attend_sigm_kb_gate_srtq256n1024t2048_kernel(
                 )
 
         def keys(u):
-            kw_got = [keep.tile([P, PACK, HALF], U32, name="kw_got%d%d" % (u, j), tag="got%d" % (j * (u + 1))) for j in range(2)]
+            kw_got = [keep.tile([P, PACK, HALF], U32, name="kw_got%d%d" % (u, j)) for j in range(2)]
             for j in range(2):
                 first = u * COLS + j * COLS // 2
                 nc.vector.tensor_copy(
@@ -226,16 +226,27 @@ def tile_attend_sigm_kb_gate_srtq256n1024t2048_kernel(
         to_columns(kb_got, kb_col, 0)
         nc.sync.dma_start(v_win[:, AHEAD:REACH], vT[:, AHEAD:REACH])
         row_gather(kb_win, kb_got, 1)
-        spare = psum.tile([P, PACK, P], F32, name="spare", tag="bank11")
-        for t in range(PACK):
+        spare = psum.tile([P, 2, P], F32, name="spare", tag="bank11")
+        for t in range(2):
             nc.tensor.transpose(spare[:, t, :], kb_got[1][:, t * P : (t + 1) * P], ident[:])
         to_columns(kb_got, kb_col, 1)
         nc.sync.dma_start(v_win[:, REACH:], vT[:, REACH:])
         keys(0)
-        vs_got.append(keep.tile([P, PASS], F32, name="vs_got1", tag="got1"))
+        vs_got.append(keep.tile([P, PASS], F32, name="vs_got1", tag="kw_got00"))
         row_gather(vs_win, vs_got, 1)
         to_columns(vs_got, vs_col, 1)
         nc.sync.dma_start(og_raw[:], og[0].rearrange("(h p) e -> p h e", p=P))
+        spare_scores = psum.tile([P, NQ + P], F32, name="spare_scores", tag="turn0")
+        for first, width in ((0, NQ), (NQ, P)):
+            nc.tensor.matmul_mx(
+                out=spare_scores[:, first : first + width],
+                lhsT=k_codes[0][:, 0, : 2 * P].bitcast(FP4X4),
+                lhsT_scale=q_plane[:, 0, :P],
+                rhs=q_codes[:, 0, :width].bitcast(FP8X4),
+                rhs_scale=q_plane[:, 0, :width],
+                start=True,
+                stop=True,
+            )
         keys(1)
         scores(0, 0, (0,), "single")
         scores(0, 0, (1,), "pair0")

from contextlib import ExitStack

import concourse.mybir as mybir
from concourse.masks import make_identity

N, T, D, DV, NQ = 1024, 2048, 1024, 128, 256
FLOPS = 2 * NQ * N * (D + DV)

F32 = mybir.dt.float32
BF16 = mybir.dt.bfloat16
I32 = mybir.dt.int32
U32 = mybir.dt.uint32
U16 = mybir.dt.uint16
U8 = mybir.dt.uint8
FP8X4 = mybir.dt.float8_e4m3fn_x4
FP4X4 = mybir.dt.float4_e2m1fn_x4
MULT = mybir.AluOpType.mult
SIGMOID = mybir.ActivationFunctionType.Sigmoid
COPY = mybir.ActivationFunctionType.Copy

P = 128
PACK = 4
PASS = P * PACK
DP = D // PASS
SP = N // PASS
QH = NQ // P
COLS = PASS // 16
REACH = T - N + PASS
ROW = P - 1
KS0 = 96
HALF = P // 2
VS_CUT = 1152
AHEAD = 320


def tile_attend_sigm_kb_gate_srtq256n1024t2048_kernel(
    tc, q_words, q_scales, k_words, k_scales, vT, vs, kb, og, offs, out
):
    nc = tc.nc
    with ExitStack() as ctx:
        keep = ctx.enter_context(tc.tile_pool(name="keep", bufs=1))
        shared = ctx.enter_context(tc.tile_pool(name="shared", bufs=1))
        psum = ctx.enter_context(tc.psum_pool(name="psum", bufs=1))

        offsets = keep.tile([P, N // 16], U16, name="offsets")
        kw_win = keep.tile([P, T], U32, name="kw_win", align_bytes=256)
        ks_win = keep.tile([P, T], U8, name="ks_win")
        kb_win = keep.tile([P, T], F32, name="kb_win")
        vs_win = keep.tile([P, T], F32, name="vs_win")
        v_win = shared.tile([P, T], F32, name="v_win", align_bytes=256, offset=0)
        q_codes = keep.tile([P, DP, NQ], U32, name="q_codes", align_bytes=256)
        q_plane = keep.tile([P, DP, NQ], U8, name="q_plane", align_bytes=64)
        k_plane = keep.tile([P, DP, N], U8, name="k_plane", align_bytes=64)
        og_raw = keep.tile([P, QH, DV], F32, name="og_raw")
        gate = keep.tile([P, QH, DV], F32, name="gate")
        ident = keep.tile([P, P], F32, name="ident")
        warm = keep.tile([P, 2], F32, name="warm")

        def zero_odd(words, zero):
            cut = words.shape[1] // 2 - 1
            nc.vector.memset(words[:, :cut], zero)
            nc.vector.memset(words[:, cut:], zero)

        nc.vector.memset(warm[:, 0:1], 0.0)
        nc.scalar.activation(warm[:, 1:2], warm[:, 0:1], SIGMOID)
        zero_odd(ks_win[:KS0, :].bitcast(I32), 0)
        zero_odd(vs_win[:ROW, :VS_CUT], 0.0)
        nc.gpsimd.memset(q_plane[:].rearrange("p o q -> p (o q)").bitcast(I32), 0)
        nc.gpsimd.memset(vs_win[:ROW, VS_CUT:REACH], 0.0)
        nc.gpsimd.memset(kb_win[:ROW, :REACH], 0.0)
        make_identity(nc, ident[:])
        nc.gpsimd.memset(k_plane[:].rearrange("p o n -> p (o n)").bitcast(I32), 0)
        nc.gpsimd.memset(kb_win[:ROW, REACH:], 0.0)
        nc.gpsimd.memset(vs_win[:ROW, REACH:], 0.0)

        k_rows = k_words[0].rearrange("p t b -> p (t b)").bitcast(I32)
        nc.sync.dma_start(ks_win[KS0:, :].bitcast(I32), k_scales.rearrange("o f t -> f o t").bitcast(I32))
        nc.sync.dma_start(offsets[:], offs)
        nc.sync.dma_start(vs_win[ROW:, :], vs[0:1, :])
        nc.sync.dma_start(kb_win[ROW:, :], kb[0:1, :])
        nc.sync.dma_start(kw_win[:, :REACH].bitcast(I32), k_rows[:, :REACH])
        for quad in range(4):
            nc.sync.dma_start(
                q_plane[32 * quad : 32 * quad + 4, :, :].bitcast(I32),
                q_scales[0][:, 4 * quad : 4 * quad + 4, :].rearrange("o f q -> f o q").bitcast(I32),
            )
        nc.sync.dma_start(q_codes[:].bitcast(I32), q_words[0].rearrange("o p q r -> p o (q r)").bitcast(I32))
        nc.sync.dma_start(kw_win[:, REACH:].bitcast(I32), k_rows[:, REACH:])
        nc.sync.dma_start(v_win[:, :AHEAD], vT[:, :AHEAD])

        def lists(u):
            return offsets[:, u * COLS : (u + 1) * COLS]

        ks_got = keep.tile([P, N], U8, name="ks_got")
        k_codes = [keep.tile([P, DP, 2 * PASS], U8, name="k_codes%d" % u, tag="codes%d" % u, align_bytes=64) for u in range(SP)]
        kb_got = [keep.tile([P, PASS], F32, name="kb_got%d" % u) for u in range(SP)]
        vs_got = [keep.tile([P, PASS], F32, name="vs_got0")]
        kb_col = [keep.tile([P, PACK], F32, name="kb_col%d" % u) for u in range(SP)]
        vs_col = [None, keep.tile([P, PACK], F32, name="vs_col1")]
        v_got = [keep.tile([P, PASS], BF16, name="v_got%d" % u) for u in range(SP)]
        prob = [
            [keep.tile([P, PACK, P], F32, name="prob00"), keep.tile([P, PACK, P], F32, name="prob01")],
            [keep.tile([P, PACK, P], F32, name="prob10"), keep.tile([P, PACK, P], F32, name="prob11")],
        ]
        w_bf = [[keep.tile([P, P, PACK], BF16, name="w_bf%d%d" % (u, h), align_bytes=64) for h in range(QH)] for u in range(SP)]
        w_codes = [
            shared.tile([P, NQ], U32, name="w_codes0", offset=4 * PASS),
            keep.tile([P, NQ], U32, name="w_codes1", align_bytes=64),
        ]
        w_plane = [keep.tile([P, NQ], U8, name="w_plane%d" % u, align_bytes=64) for u in range(SP)]
        v_bf = [keep.tile([P, DV, PACK], BF16, name="v_bf%d" % u, align_bytes=64) for u in range(SP)]
        v_codes = [keep.tile([P, DV], U32, name="v_codes%d" % u, align_bytes=64) for u in range(SP)]
        v_plane = [keep.tile([P, DV], U8, name="v_plane%d" % u, align_bytes=64) for u in range(SP)]
        result = [keep.tile([P, DV], F32, name="result%d" % h) for h in range(QH)]

        def row_gather(win, got, u):
            nc.scalar.activation(got[u][:], win[:, : (REACH, T)[u]].indirect(lists(u)), COPY)

        def to_columns(got, col, u):
            nc.sync.dma_start(col[u][:], got[u][ROW:, :].rearrange("o (p t) -> o p t", t=PACK))

        def key_scales():
            nc.vector.tensor_copy(
                ks_got[:].rearrange("g (u t p) -> g u p t", u=SP, t=PACK), ks_win[:].indirect(offsets[:])
            )

        def scale_moves():
            for quad in (0, 2, 1, 3):
                nc.sync.dma_start(
                    k_plane[32 * quad : 32 * quad + 4, :, :].bitcast(I32),
                    ks_got[KS0 + 8 * quad : KS0 + 8 * quad + 8, :].bitcast(I32),
                )

        def keys(u):
            kw_got = [keep.tile([P, PACK, HALF], U32, name="kw_got%d%d" % (u, j)) for j in range(2)]
            for j in range(2):
                first = u * COLS + j * COLS // 2
                nc.vector.tensor_copy(
                    kw_got[j][:].rearrange("g t p -> g p t"),
                    kw_win[:, : (REACH, T)[u]].indirect(offsets[:, first : first + COLS // 2]),
                )
            for j in range(2):
                nc.vector.tensor_copy(
                    k_codes[u][:].bitcast(U16).rearrange("g o (t p) -> g o t p", t=PACK)[
                        :, :, :, j * HALF : (j + 1) * HALF
                    ],
                    kw_got[j][:]
                    .rearrange("g t p -> g (t p)")
                    .bitcast(U16)
                    .rearrange("g (t p o) -> g o t p", t=PACK, o=DP),
                )

        def scores(u, h, places, tag):
            cols = slice(h * P, (h + 1) * P)
            bank = psum.tile([P, len(places), P], F32, name="bank%d%d%d" % (u, h, places[0]), tag=tag)
            for o in range(DP):
                for j, t in enumerate(places):
                    nc.tensor.matmul_mx(
                        out=bank[:, j, :],
                        lhsT=k_codes[u][:, o, 2 * P * t : 2 * P * (t + 1)].bitcast(FP4X4),
                        lhsT_scale=k_plane[:, o, PASS * u + P * t : PASS * u + P * (t + 1)],
                        rhs=q_codes[:, o, cols].bitcast(FP8X4),
                        rhs_scale=q_plane[:, o, cols],
                        start=(o == 0 and j == 0),
                        stop=(o == DP - 1 and j == len(places) - 1),
                    )
            for j, t in enumerate(places):
                nc.scalar.activation(prob[u][h][:, t, :], bank[:, j, :], SIGMOID, bias=kb_col[u][:, t : t + 1])

        def turn_values(u):
            turned = psum.tile([P, 2, DV], F32, name="turned%d" % u, tag="turn%d" % u)
            words = v_got[u][:].bitcast(F32)
            for j in range(2):
                nc.tensor.transpose(turned[:, j, :], words[:, j::2], ident[:])
            return turned

        def copy_values(u, turned):
            nc.scalar.copy(
                v_bf[u][:].rearrange("p e t -> p (e t)").bitcast(F32).rearrange("p (e j) -> p e j", j=2),
                turned[:].rearrange("p j e -> p e j"),
            )

        def weights(u, h):
            nc.vector.tensor_tensor(
                w_bf[u][h][:].rearrange("p (c i) t -> p c t i", i=4),
                prob[u][h][:].rearrange("p t (c i) -> p c t i", i=4),
                (vs_turned[:, :, ROW], vs_col[1][:])[u].unsqueeze(1).unsqueeze(3).to_broadcast([P, P // 4, PACK, 4]),
                MULT,
            )

        def quantise_v(u):
            nc.vector.quantize_mx(
                out=v_codes[u][:].bitcast(FP8X4), scales=v_plane[u][:], in_=v_bf[u][:].rearrange("p e t -> p (e t)")
            )

        def quantise_w(u, h):
            cols = slice(h * P, (h + 1) * P)
            nc.vector.quantize_mx(
                out=w_codes[u][:, cols].bitcast(FP8X4),
                scales=w_plane[u][:, cols],
                in_=w_bf[u][h][:].rearrange("p q t -> p (q t)"),
            )

        def finish(h, order):
            acc = psum.tile([P, DV], F32, name="acc%d" % h, tag="acc%d" % h)
            for step, u in enumerate(order):
                nc.tensor.matmul_mx(
                    out=acc[:],
                    lhsT=w_codes[u][:, h * P : (h + 1) * P].bitcast(FP8X4),
                    lhsT_scale=w_plane[u][:, h * P : (h + 1) * P],
                    rhs=v_codes[u][:].bitcast(FP8X4),
                    rhs_scale=v_plane[u][:],
                    start=(step == 0),
                    stop=(step == SP - 1),
                )
            nc.vector.scalar_tensor_tensor(result[h][:], acc[:], 1.0 / 16.0, gate[:, h, :], MULT, MULT)
            nc.sync.dma_start(out[0, h * P : (h + 1) * P, :], result[h][:])

        row_gather(vs_win, vs_got, 0)
        row_gather(kb_win, kb_got, 0)
        vs_turned = psum.tile([P, PACK, P], F32, name="vs_turned", tag="turn1")
        for t in range(PACK):
            nc.tensor.transpose(vs_turned[:, t, :], vs_got[0][:, t::PACK], ident[:])
        key_scales()
        scale_moves()
        to_columns(kb_got, kb_col, 0)
        nc.sync.dma_start(v_win[:, AHEAD:REACH], vT[:, AHEAD:REACH])
        row_gather(kb_win, kb_got, 1)
        spare = psum.tile([P, 2, P], F32, name="spare", tag="bank11")
        for t in range(2):
            nc.tensor.transpose(spare[:, t, :], kb_got[1][:, t * P : (t + 1) * P], ident[:])
        to_columns(kb_got, kb_col, 1)
        nc.sync.dma_start(v_win[:, REACH:], vT[:, REACH:])
        keys(0)
        vs_got.append(keep.tile([P, PASS], F32, name="vs_got1", tag="kw_got00"))
        row_gather(vs_win, vs_got, 1)
        to_columns(vs_got, vs_col, 1)
        nc.sync.dma_start(og_raw[:], og[0].rearrange("(h p) e -> p h e", p=P))
        spare_scores = psum.tile([P, NQ + P], F32, name="spare_scores", tag="turn0")
        for first, width in ((0, NQ), (NQ, P)):
            nc.tensor.matmul_mx(
                out=spare_scores[:, first : first + width],
                lhsT=k_codes[0][:, 0, : 2 * P].bitcast(FP4X4),
                lhsT_scale=q_plane[:, 0, :P],
                rhs=q_codes[:, 0, :width].bitcast(FP8X4),
                rhs_scale=q_plane[:, 0, :width],
                start=True,
                stop=True,
            )
        keys(1)
        scores(0, 0, (0,), "single")
        scores(0, 0, (1,), "pair0")
        scores(0, 0, (2, 3), "pair1")
        scores(0, 1, (0, 1), "acc0")
        scores(0, 1, (2, 3), "acc1")
        weights(0, 0)
        weights(0, 1)
        nc.vector.tensor_copy(v_got[0][:], v_win[:].indirect(lists(0)))
        scores(1, 0, (0, 1), "pair0")
        scores(1, 0, (2, 3), "pair1")
        nc.scalar.activation(v_got[1][:], v_win[:].indirect(lists(1)), COPY)
        weights(1, 0)
        quantise_w(0, 0)
        quantise_w(0, 1)
        scores(1, 1, range(PACK), "bank11")
        turned = [turn_values(u) for u in range(SP)]
        for u in range(SP):
            copy_values(u, turned[u])
        nc.scalar.activation(gate[:], og_raw[:], SIGMOID)
        quantise_w(1, 0)
        weights(1, 1)
        quantise_v(0)
        quantise_v(1)
        quantise_w(1, 1)
        finish(0, (0, 1))
        finish(1, (0, 1))
